import numpy as np
import ml_dtypes


def mxq(x, axis, fmt="e4m3"):
    dtype, down = {"e4m3": (ml_dtypes.float8_e4m3fn, 7), "e5m2": (ml_dtypes.float8_e5m2, 14)}[fmt]
    v = np.moveaxis(np.asarray(x, np.float32).astype(ml_dtypes.bfloat16).astype(np.float64), axis, -1)
    blocks = v.reshape(v.shape[:-1] + (-1, 32))
    amax = np.abs(blocks).max(-1, keepdims=True)
    byte = np.maximum(np.where(amax > 0, np.frexp(amax)[1] - 1 + 127, 0) - down, 1)
    scale = np.exp2(byte - 127.0)
    codes = (blocks / scale).astype(np.float32).astype(dtype).astype(np.float64)
    return np.moveaxis((codes * scale).reshape(v.shape), -1, axis)


WIDE = False


def mx_kscale(k):
    if not WIDE:
        return np.ones(k)
    levels = np.array([10, -10, 5, -5, 0])
    if k % 512:
        return np.exp2(np.random.permutation(np.resize(levels, k // 32))).repeat(32)
    a = np.empty((k // 512, 16))
    for p in range(k // 512):
        a[p, :8] = np.random.permutation(np.resize(levels, 8))
        for g in range(8):
            far = levels[np.abs(levels - a[p, g]) >= 10]
            a[p, g + 8] = far[np.random.randint(len(far))]
    return np.exp2(a.ravel()).repeat(32)


def f64(x):
    return np.asarray(x).astype(np.float64)


def striped(idx):
    return np.tile(idx.reshape(-1, 16).T, (8, 1)).astype(np.uint16)


def unstriped(offs):
    return offs[:16].T.reshape(-1).astype(np.int64)


def pack_weight(w):
    k, n = w.shape
    w = f64(np.asarray(w, np.float32).astype(ml_dtypes.bfloat16)).reshape(k // 32, 32, n)
    amax = np.abs(w).max(1)
    byte = np.clip(np.where(amax > 0, np.frexp(amax)[1] - 1 + 127 - 7, 1), 1, 254)
    scaled = (w * np.exp2(127.0 - byte)[:, None, :]).reshape(k, n).astype(np.float32)
    words = np.ascontiguousarray(scaled.reshape(k // 512, 128, 4, n).transpose(0, 1, 3, 2)).astype(ml_dtypes.float8_e4m3fn).view(np.uint8)
    return words, np.ascontiguousarray(byte.astype(np.uint8).reshape(k // 512, 16, n))


def unpack_weight(words, scales):
    g, p, n, _ = words.shape
    vals = np.ascontiguousarray(words).view(ml_dtypes.float8_e4m3fn).astype(np.float64) * np.repeat(np.exp2(scales.astype(np.float64) - 127.0), 8, axis=1)[..., None]
    return vals.transpose(0, 1, 3, 2).reshape(g * 512, n)


K, T, S, H, N, U = 1024, 2048, 512, 512, 128, 1024


def setup_inputs():
    n = np.random.standard_normal
    s = mx_kscale(K)[:, None]
    u = mx_kscale(H)
    packed_xT = pack_weight(n((K, T)) * s)
    return {
        "x_words": packed_xT[0],
        "x_scales": packed_xT[1],
        "mom": (n((N, U))).astype(np.float32),
        "w1": (n((K, H)) / np.sqrt(K) / s).astype(np.float32),
        "w2": (n((H, N)) / np.sqrt(H) / u[:, None]).astype(np.float32),
        "bias": (0.5 * n((H, 1))).astype(np.float32),
        "top": (n((H, 1)) * u[:, None]).astype(np.float32),
        "drag": (np.random.uniform(0.8, 1.0, (N, 1))).astype(np.float32),
        "offs": striped(np.random.permutation(T)[:S]),
        "slot": striped(np.random.permutation(U)[:S]),
    }


def reference(x_words, x_scales, mom, w1, w2, bias, top, drag, offs, slot):
    xq = unpack_weight(x_words, x_scales)[:, unstriped(offs)]
    h = np.tanh((mxq(f64(w1), 0, "e4m3").T @ xq) + f64(bias))
    z = f64(top) * (-1.0 * ((h) ** 2) + 1.0)
    p = f64(mom)[:, unstriped(slot)] - (0.4 * ((mxq(f64(w2), 0, "e4m3").T @ mxq(z, 0, "e4m3"))))
    out = f64(mom).copy()
    out[:, unstriped(slot)] = f64(drag) * p
    return out

@@ -1,0 +1,167 @@
+from contextlib import ExitStack
+
+import concourse.mybir as mybir
+
+K, T, S, H, N, U = 1024, 2048, 512, 512, 128, 1024
+FLOPS = 2 * K * H * S + 2 * H * N * S
+
+F32 = mybir.dt.float32
+BF16 = mybir.dt.bfloat16
+I32 = mybir.dt.int32
+U32 = mybir.dt.uint32
+U16 = mybir.dt.uint16
+U8 = mybir.dt.uint8
+FP8X4 = mybir.dt.float8_e4m3fn_x4
+ACT = mybir.ActivationFunctionType
+ALU = mybir.AluOpType
+
+P = 128
+PACK = 4
+PASSES = K // (P * PACK)
+HALF = 256
+CHUNK = 128
+KICK = 0.4
+
+
+def tile_picked_yham_drag_p_kernel(tc, x_words, x_scales, mom, w1, w2, bias, top, drag, offs, slot, out):
+    nc = tc.nc
+    with ExitStack() as ctx:
+        sb = ctx.enter_context(tc.tile_pool(name="sb", bufs=1))
+        ps = ctx.enter_context(tc.psum_pool(name="ps", bufs=1))
+
+        def tile(shape, dtype, name, tag=None):
+            return sb.tile(shape, dtype, name=name, tag=tag or name, align_bytes=64)
+
+        offs_t = sb.tile([P, S // 16], U16, name="offs_t")
+        slot_t = sb.tile([P, S // 16], U16, name="slot_t")
+        w1_raw = [tile([P, PACK, H], F32, f"w1_raw{g}") for g in range(PASSES)]
+        xw = [tile([P, T], U32, f"xw{g}") for g in range(PASSES)]
+        xs = tile([P, T], U8, "xs")
+        window = tile([P, U], F32, "window")
+        w2_raw = tile([P, PACK, N], F32, "w2_raw")
+        bias_t = tile([P, PACK], F32, "bias_t")
+        top_t = tile([P, PACK], F32, "top_t")
+        drag_t = tile([P, 1], F32, "drag_t")
+
+        def load_w1(g):
+            nc.sync.dma_start(out=w1_raw[g][:], in_=w1[g * 512:(g + 1) * 512, :].rearrange("(p j) c -> p j c", j=PACK))
+
+        def load_x(g):
+            nc.sync.dma_start(out=xw[g][:].bitcast(I32), in_=x_words[g].rearrange("p n t -> p (n t)").bitcast(I32))
+
+        def load_scales(engine):
+            for q in range(4):
+                engine.dma_start(out=xs[32 * q:32 * q + 4 * PASSES, :].bitcast(I32),
+                                 in_=x_scales[:, 4 * q:4 * q + 4, :].bitcast(I32))
+
+        def load_w2():
+            nc.sync.dma_start(out=w2_raw[:], in_=w2.rearrange("(p j) n -> p j n", j=PACK))
+
+        nc.vector.memset(xs[:].bitcast(I32), 0)
+        load_w1(0)
+        load_scales(nc.sync)
+        nc.sync.dma_start(offs_t[:], offs)
+        load_w1(1)
+        load_x(0)
+        load_w2()
+        load_x(1)
+        nc.sync.dma_start(slot_t[:], slot)
+        nc.sync.dma_start(out=window[:], in_=mom)
+        nc.gpsimd.dma_start(out=bias_t[:], in_=bias.rearrange("(p t) o -> p (t o)", t=PACK))
+        nc.gpsimd.dma_start(out=top_t[:], in_=top.rearrange("(p t) o -> p (t o)", t=PACK))
+        nc.gpsimd.dma_start(out=drag_t[:], in_=drag)
+
+        warm = tile([P, 1], F32, "warm")
+        warm_in = tile([P, 1], F32, "warm_in")
+        nc.vector.memset(warm_in[:], 0.0)
+        nc.scalar.activation(warm[:], warm_in[:], ACT.Tanh)
+
+        kick = tile([P, 1], F32, "kick")
+        nc.gpsimd.tensor_scalar(kick[:], drag_t[:], -KICK, None, ALU.mult)
+
+        w1_c = [tile([P, H], U32, f"w1_c{g}") for g in range(PASSES)]
+        w1_s = [tile([P, H], U8, f"w1_s{g}") for g in range(PASSES)]
+        gs = tile([P, S], U8, "gs")
+
+        for g in range(PASSES):
+            src = w1_raw[g][:].rearrange("p j (m u t) -> p u m t j", u=2, t=2)
+            w1_b = [tile([P, 2 * P * PACK], BF16, f"w1_b{g}_{u}") for u in range(2)]
+            dst = [w1_b[u][:].rearrange("p (t m j) -> p m t j", t=2, j=PACK) for u in range(2)]
+            nc.vector.tensor_copy(dst[0], src[:, 0])
+            nc.scalar.copy(dst[1], src[:, 1])
+            if g == 0:
+                nc.vector.tensor_copy(gs[:], xs[:].indirect(offs_t[:]))
+            for u in range(2):
+                cols = slice(u * 2 * P, (u + 1) * 2 * P)
+                nc.vector.quantize_mx(out=w1_c[g][:, cols].bitcast(FP8X4), scales=w1_s[g][:, cols], in_=w1_b[u][:])
+
+        w2_b = tile([P, N * PACK], BF16, "w2_b")
+        w2_c = tile([P, N], U32, "w2_c")
+        w2_s = tile([P, N], U8, "w2_s")
+
+        def quantize_w2():
+            nc.scalar.copy(w2_b[:].rearrange("p (n j) -> p n j", j=PACK), w2_raw[:].rearrange("p j n -> p n j"))
+            nc.vector.quantize_mx(out=w2_c[:].bitcast(FP8X4), scales=w2_s[:], in_=w2_b[:])
+
+        halves = S // HALF
+        gx = [[tile([P, HALF], U32, f"gx{g}_{a}") for a in range(halves)] for g in range(PASSES)]
+        banks = [[ps.tile([P, HALF], F32, name=f"pre{a}_{t}", tag=f"bank{a}_{t}") for t in range(PACK)] for a in range(halves)]
+        for g in range(PASSES):
+            for a in range(halves):
+                nc.vector.tensor_copy(gx[g][a][:], xw[g][:].indirect(offs_t[:, a * HALF // 16:(a + 1) * HALF // 16]))
+                for t in range(PACK):
+                    nc.tensor.matmul_mx(
+                        out=banks[a][t][:],
+                        lhsT=w1_c[g][:, t * P:(t + 1) * P].bitcast(FP8X4),
+                        lhsT_scale=w1_s[g][:, t * P:(t + 1) * P],
+                        rhs=gx[g][a][:].bitcast(FP8X4),
+                        rhs_scale=gs[4 * g:P, a * HALF:(a + 1) * HALF],
+                        start=(g == 0), stop=(g == PASSES - 1))
+            if g == 0:
+                quantize_w2()
+
+        mom_g = tile([P, S], F32, "mom_g")
+        nc.vector.tensor_copy(mom_g[:], window[:].indirect(slot_t[:]))
+        kept = tile([P, S], F32, "kept")
+        nc.vector.tensor_scalar(kept[:], mom_g[:], drag_t[:], None, ALU.mult)
+
+        neg_top = tile([P, PACK], F32, "neg_top", "mom_g")
+        nc.vector.tensor_scalar(neg_top[:], top_t[:], -1.0, None, ALU.mult)
+
+        chunks = S // CHUNK
+        per_half = HALF // CHUNK
+        z_c = [tile([P, CHUNK], U32, f"z_c{c}") for c in range(chunks)]
+        z_s = [tile([P, CHUNK], U8, f"z_s{c}") for c in range(chunks)]
+        kicked = [tile([P, CHUNK], F32, f"kicked{c}") for c in range(chunks)]
+
+        def hidden(c):
+            a, b = divmod(c, per_half)
+            h = tile([P, PACK, CHUNK], F32, f"h{c}", f"hh{c - 2}" if c >= 2 else None)
+            hh = tile([P, CHUNK, PACK], F32, f"hh{c}")
+            z_b = tile([P, CHUNK, PACK], BF16, f"z_b{c}", "z_b")
+            for t in range(PACK):
+                nc.scalar.activation(h[:, t, :], banks[a][t][:, b * CHUNK:(b + 1) * CHUNK], ACT.Tanh,
+                                     bias=bias_t[:, t:t + 1])
+            nc.scalar.activation(hh[:], h[:].rearrange("p t j -> p j t"), ACT.Square)
+            nc.vector.scalar_tensor_tensor(z_b[:], hh[:], 1.0,
+                                           neg_top[:].unsqueeze(1).to_broadcast([P, CHUNK, PACK]),
+                                           ALU.subtract, ALU.mult)
+            nc.vector.quantize_mx(out=z_c[c][:].bitcast(FP8X4), scales=z_s[c][:],
+                                  in_=z_b[:].rearrange("p j t -> p (j t)"))
+
+        def finish(c):
+            y = ps.tile([P, CHUNK], F32, name=f"y{c}", tag=f"bank0_{c}")
+            nc.tensor.matmul_mx(out=y[:], lhsT=w2_c[:].bitcast(FP8X4), lhsT_scale=w2_s[:],
+                                rhs=z_c[c][:].bitcast(FP8X4), rhs_scale=z_s[c][:], start=True, stop=True)
+            nc.scalar.activation(kicked[c][:], y[:], ACT.Copy, scale=kick[:])
+            nc.vector.tensor_tensor(window[:].indirect(slot_t[:, c * CHUNK // 16:(c + 1) * CHUNK // 16]),
+                                    kept[:, c * CHUNK:(c + 1) * CHUNK], kicked[c][:], ALU.add)
+
+        for c in range(chunks + 1):
+            if c < chunks:
+                hidden(c)
+            if c > 0:
+                finish(c - 1)
+
+
+        nc.sync.dma_start(out=out, in_=window[:])

@@ -57,27 +57,29 @@ def tile_picked_yham_drag_p_kernel(tc, x_words, x_scales, mom, w1, w2, bias, top
         def load_w2():
             nc.sync.dma_start(out=w2_raw[:], in_=w2.rearrange("(p j) n -> p j n", j=PACK))
 
-        nc.vector.memset(xs[:].bitcast(I32), 0)
+        nc.gpsimd.memset(xs[:].bitcast(I32), 0)
+        load_scales(nc.gpsimd)
         load_w1(0)
-        load_scales(nc.sync)
         nc.sync.dma_start(offs_t[:], offs)
         load_w1(1)
         load_x(0)
-        load_w2()
-        load_x(1)
         nc.sync.dma_start(slot_t[:], slot)
+        load_x(1)
         nc.sync.dma_start(out=window[:], in_=mom)
-        nc.gpsimd.dma_start(out=bias_t[:], in_=bias.rearrange("(p t) o -> p (t o)", t=PACK))
-        nc.gpsimd.dma_start(out=top_t[:], in_=top.rearrange("(p t) o -> p (t o)", t=PACK))
-        nc.gpsimd.dma_start(out=drag_t[:], in_=drag)
+        load_w2()
+        nc.scalar.dma_start(out=bias_t[:], in_=bias.rearrange("(p t) o -> p (t o)", t=PACK))
+        nc.scalar.dma_start(out=top_t[:], in_=top.rearrange("(p t) o -> p (t o)", t=PACK))
+        nc.scalar.dma_start(out=drag_t[:], in_=drag)
 
         warm = tile([P, 1], F32, "warm")
         warm_in = tile([P, 1], F32, "warm_in")
         nc.vector.memset(warm_in[:], 0.0)
         nc.scalar.activation(warm[:], warm_in[:], ACT.Tanh)
 
-        kick = tile([P, 1], F32, "kick")
-        nc.gpsimd.tensor_scalar(kick[:], drag_t[:], -KICK, None, ALU.mult)
+        neg_top = tile([P, PACK], F32, "neg_top")
+        nc.vector.tensor_scalar(neg_top[:], top_t[:], -1.0, None, ALU.mult)
+        drag_wide = tile([P, CHUNK], F32, "drag_wide")
+        nc.scalar.copy(drag_wide[:], drag_t[:].to_broadcast([P, CHUNK]))
 
         w1_c = [tile([P, H], U32, f"w1_c{g}") for g in range(PASSES)]
         w1_s = [tile([P, H], U8, f"w1_s{g}") for g in range(PASSES)]
@@ -100,7 +102,7 @@ def tile_picked_yham_drag_p_kernel(tc, x_words, x_scales, mom, w1, w2, bias, top
         w2_s = tile([P, N], U8, "w2_s")
 
         def quantize_w2():
-            nc.scalar.copy(w2_b[:].rearrange("p (n j) -> p n j", j=PACK), w2_raw[:].rearrange("p j n -> p n j"))
+            nc.vector.tensor_copy(w2_b[:].rearrange("p (n j) -> p n j", j=PACK), w2_raw[:].rearrange("p j n -> p n j"))
             nc.vector.quantize_mx(out=w2_c[:].bitcast(FP8X4), scales=w2_s[:], in_=w2_b[:])
 
         halves = S // HALF
@@ -117,51 +119,51 @@ def tile_picked_yham_drag_p_kernel(tc, x_words, x_scales, mom, w1, w2, bias, top
                         rhs=gx[g][a][:].bitcast(FP8X4),
                         rhs_scale=gs[4 * g:P, a * HALF:(a + 1) * HALF],
                         start=(g == 0), stop=(g == PASSES - 1))
-            if g == 0:
-                quantize_w2()
 
         mom_g = tile([P, S], F32, "mom_g")
         nc.vector.tensor_copy(mom_g[:], window[:].indirect(slot_t[:]))
-        kept = tile([P, S], F32, "kept")
-        nc.vector.tensor_scalar(kept[:], mom_g[:], drag_t[:], None, ALU.mult)
+        quantize_w2()
 
-        neg_top = tile([P, PACK], F32, "neg_top", "mom_g")
-        nc.vector.tensor_scalar(neg_top[:], top_t[:], -1.0, None, ALU.mult)
+        chunks = [(0, 128), (128, 128), (256, 128), (384, 128)]
+        tanh_runs = {0: 128, 128: 128, 256: 128, 384: 128}
 
-        chunks = S // CHUNK
-        per_half = HALF // CHUNK
-        z_c = [tile([P, CHUNK], U32, f"z_c{c}") for c in range(chunks)]
-        z_s = [tile([P, CHUNK], U8, f"z_s{c}") for c in range(chunks)]
-        kicked = [tile([P, CHUNK], F32, f"kicked{c}") for c in range(chunks)]
-
-        def hidden(c):
-            a, b = divmod(c, per_half)
-            h = tile([P, PACK, CHUNK], F32, f"h{c}", f"hh{c - 2}" if c >= 2 else None)
-            hh = tile([P, CHUNK, PACK], F32, f"hh{c}")
-            z_b = tile([P, CHUNK, PACK], BF16, f"z_b{c}", "z_b")
+        def tanh_run(start, size):
+            a, b = divmod(start, HALF)
+            h = tile([P, PACK, size], F32, f"h{start}")
             for t in range(PACK):
-                nc.scalar.activation(h[:, t, :], banks[a][t][:, b * CHUNK:(b + 1) * CHUNK], ACT.Tanh,
-                                     bias=bias_t[:, t:t + 1])
-            nc.scalar.activation(hh[:], h[:].rearrange("p t j -> p j t"), ACT.Square)
+                nc.scalar.activation(h[:, t, :], banks[a][t][:, b:b + size], ACT.Tanh, bias=bias_t[:, t:t + 1])
+            return h
+
+        def hidden(start, size, h):
+            hh = tile([P, size, PACK], F32, f"hh{start}")
+            z_b = tile([P, size, PACK], BF16, f"z_b{start}", "w2_raw")
+            z_c = tile([P, size], U32, f"z_c{start}")
+            z_s = tile([P, size], U8, f"z_s{start}")
+            nc.scalar.activation(hh[:], h.rearrange("p t j -> p j t"), ACT.Square)
             nc.vector.scalar_tensor_tensor(z_b[:], hh[:], 1.0,
-                                           neg_top[:].unsqueeze(1).to_broadcast([P, CHUNK, PACK]),
+                                           neg_top[:].unsqueeze(1).to_broadcast([P, size, PACK]),
                                            ALU.subtract, ALU.mult)
-            nc.vector.quantize_mx(out=z_c[c][:].bitcast(FP8X4), scales=z_s[c][:],
-                                  in_=z_b[:].rearrange("p j t -> p (j t)"))
+            nc.vector.quantize_mx(out=z_c[:].bitcast(FP8X4), scales=z_s[:], in_=z_b[:].rearrange("p j t -> p (j t)"))
+            return z_c, z_s
 
-        def finish(c):
-            y = ps.tile([P, CHUNK], F32, name=f"y{c}", tag=f"bank0_{c}")
+        def finish(c, start, size, z_c, z_s):
+            y = ps.tile([P, size], F32, name=f"y{c}", tag=f"bank{c // PACK}_{c % PACK}")
             nc.tensor.matmul_mx(out=y[:], lhsT=w2_c[:].bitcast(FP8X4), lhsT_scale=w2_s[:],
-                                rhs=z_c[c][:].bitcast(FP8X4), rhs_scale=z_s[c][:], start=True, stop=True)
-            nc.scalar.activation(kicked[c][:], y[:], ACT.Copy, scale=kick[:])
-            nc.vector.tensor_tensor(window[:].indirect(slot_t[:, c * CHUNK // 16:(c + 1) * CHUNK // 16]),
-                                    kept[:, c * CHUNK:(c + 1) * CHUNK], kicked[c][:], ALU.add)
+                                rhs=z_c[:].bitcast(FP8X4), rhs_scale=z_s[:], start=True, stop=True)
+            p = tile([P, size], F32, f"p{c}", f"h{start + size}" if start + size < S else None)
+            nc.vector.scalar_tensor_tensor(p[:], y[:], -KICK, mom_g[:, start:start + size], ALU.mult, ALU.add)
+            nc.vector.tensor_tensor(window[:].indirect(slot_t[:, start // 16:(start + size) // 16]),
+                                    p[:], drag_wide[:, :size], ALU.mult)
 
-        for c in range(chunks + 1):
-            if c < chunks:
-                hidden(c)
-            if c > 0:
-                finish(c - 1)
+        pending = None
+        for c, (start, size) in enumerate(chunks):
+            if start in tanh_runs:
+                run_start, h = start, tanh_run(start, tanh_runs[start])
+            made = hidden(start, size, h[:, :, start - run_start:start - run_start + size])
+            if pending:
+                finish(*pending)
+            pending = (c, start, size, *made)
+        finish(*pending)
 
 
         nc.sync.dma_start(out=out, in_=window[:])

@@ -57,19 +57,19 @@ def tile_picked_yham_drag_p_kernel(tc, x_words, x_scales, mom, w1, w2, bias, top
         def load_w2():
             nc.sync.dma_start(out=w2_raw[:], in_=w2.rearrange("(p j) n -> p j n", j=PACK))
 
-        nc.gpsimd.memset(xs[:].bitcast(I32), 0)
-        load_scales(nc.gpsimd)
+        nc.vector.memset(xs[:].bitcast(I32), 0)
         load_w1(0)
+        load_scales(nc.sync)
         nc.sync.dma_start(offs_t[:], offs)
         load_w1(1)
         load_x(0)
         nc.sync.dma_start(slot_t[:], slot)
         load_x(1)
+        nc.sync.dma_start(out=bias_t[:], in_=bias.rearrange("(p t) o -> p (t o)", t=PACK))
+        nc.sync.dma_start(out=top_t[:], in_=top.rearrange("(p t) o -> p (t o)", t=PACK))
+        nc.sync.dma_start(out=drag_t[:], in_=drag)
         nc.sync.dma_start(out=window[:], in_=mom)
         load_w2()
-        nc.scalar.dma_start(out=bias_t[:], in_=bias.rearrange("(p t) o -> p (t o)", t=PACK))
-        nc.scalar.dma_start(out=top_t[:], in_=top.rearrange("(p t) o -> p (t o)", t=PACK))
-        nc.scalar.dma_start(out=drag_t[:], in_=drag)
 
         warm = tile([P, 1], F32, "warm")
         warm_in = tile([P, 1], F32, "warm_in")
@@ -77,9 +77,9 @@ def tile_picked_yham_drag_p_kernel(tc, x_words, x_scales, mom, w1, w2, bias, top
         nc.scalar.activation(warm[:], warm_in[:], ACT.Tanh)
 
         neg_top = tile([P, PACK], F32, "neg_top")
-        nc.vector.tensor_scalar(neg_top[:], top_t[:], -1.0, None, ALU.mult)
+        nc.gpsimd.tensor_scalar(neg_top[:], top_t[:], -1.0, 0.0, ALU.mult, ALU.add)
         drag_wide = tile([P, CHUNK], F32, "drag_wide")
-        nc.scalar.copy(drag_wide[:], drag_t[:].to_broadcast([P, CHUNK]))
+        nc.gpsimd.tensor_scalar(drag_wide[:], drag_t[:].to_broadcast([P, CHUNK]), 1.0, 0.0, ALU.mult, ALU.add)
 
         w1_c = [tile([P, H], U32, f"w1_c{g}") for g in range(PASSES)]
         w1_s = [tile([P, H], U8, f"w1_s{g}") for g in range(PASSES)]

@@ -78,6 +78,8 @@ def tile_picked_yham_drag_p_kernel(tc, x_words, x_scales, mom, w1, w2, bias, top
 
         neg_top = tile([P, PACK], F32, "neg_top")
         nc.gpsimd.tensor_scalar(neg_top[:], top_t[:], -1.0, 0.0, ALU.mult, ALU.add)
+        kick = tile([P, 1], F32, "kick")
+        nc.gpsimd.tensor_scalar(kick[:], drag_t[:], -KICK, 0.0, ALU.mult, ALU.add)
         drag_wide = tile([P, CHUNK], F32, "drag_wide")
         nc.gpsimd.tensor_scalar(drag_wide[:], drag_t[:].to_broadcast([P, CHUNK]), 1.0, 0.0, ALU.mult, ALU.add)
 
@@ -124,8 +126,6 @@ def tile_picked_yham_drag_p_kernel(tc, x_words, x_scales, mom, w1, w2, bias, top
         nc.vector.tensor_copy(mom_g[:], window[:].indirect(slot_t[:]))
         quantize_w2()
 
-        chunks = [(0, 128), (128, 128), (256, 128), (384, 128)]
-        tanh_runs = {0: 128, 128: 128, 256: 128, 384: 128}
 
         def tanh_run(start, size):
             a, b = divmod(start, HALF)
@@ -146,24 +146,45 @@ def tile_picked_yham_drag_p_kernel(tc, x_words, x_scales, mom, w1, w2, bias, top
             nc.vector.quantize_mx(out=z_c[:].bitcast(FP8X4), scales=z_s[:], in_=z_b[:].rearrange("p j t -> p (j t)"))
             return z_c, z_s
 
-        def finish(c, start, size, z_c, z_s):
-            y = ps.tile([P, size], F32, name=f"y{c}", tag=f"bank{c // PACK}_{c % PACK}")
+        def product(c, z_c, z_s):
+            y = ps.tile([P, CHUNK], F32, name=f"y{c}", tag=f"bank0_{c}")
             nc.tensor.matmul_mx(out=y[:], lhsT=w2_c[:].bitcast(FP8X4), lhsT_scale=w2_s[:],
                                 rhs=z_c[:].bitcast(FP8X4), rhs_scale=z_s[:], start=True, stop=True)
-            p = tile([P, size], F32, f"p{c}", f"h{start + size}" if start + size < S else None)
-            nc.vector.scalar_tensor_tensor(p[:], y[:], -KICK, mom_g[:, start:start + size], ALU.mult, ALU.add)
-            nc.vector.tensor_tensor(window[:].indirect(slot_t[:, start // 16:(start + size) // 16]),
-                                    p[:], drag_wide[:, :size], ALU.mult)
+            if c < 2:
+                p = tile([P, CHUNK], F32, f"p{c}", f"h{(c + 1) * CHUNK}")
+                nc.vector.scalar_tensor_tensor(p[:], y[:], -KICK, mom_g[:, c * CHUNK:(c + 1) * CHUNK], ALU.mult, ALU.add)
+                return p[:], drag_wide[:], ALU.mult
+            kicked = tile([P, CHUNK], F32, f"kicked{c}")
+            nc.scalar.activation(kicked[:], y[:], ACT.Copy, scale=kick[:])
+            return kept[:, (c - 2) * CHUNK:(c - 1) * CHUNK], kicked[:], ALU.add
 
-        pending = None
-        for c, (start, size) in enumerate(chunks):
-            if start in tanh_runs:
-                run_start, h = start, tanh_run(start, tanh_runs[start])
-            made = hidden(start, size, h[:, :, start - run_start:start - run_start + size])
-            if pending:
-                finish(*pending)
-            pending = (c, start, size, *made)
-        finish(*pending)
+        def scatter(c, in0, in1, op):
+            nc.vector.tensor_tensor(window[:].indirect(slot_t[:, c * CHUNK // 16:(c + 1) * CHUNK // 16]), in0, in1, op)
 
+        def make_z(c):
+            return hidden(c * CHUNK, CHUNK, tanh_run(c * CHUNK, CHUNK)[:])
+
+        z0 = make_z(0)
+        z1 = make_z(1)
+        scatter(0, *product(0, *z0))
+        z2 = make_z(2)
+        r1 = product(1, *z1)
+        scatter(1, *r1)
+        h3 = tanh_run(3 * CHUNK, CHUNK)
+        hh3 = tile([P, PACK, CHUNK], F32, "hh3")
+        nc.scalar.activation(hh3[:], h3[:], ACT.Square)
+        z_rows = tile([P, PACK, CHUNK], BF16, "z_rows")
+        for t in range(PACK):
+            nc.scalar.activation(z_rows[:, t, :], hh3[:, t, :], ACT.Identity, bias=top_t[:, t:t + 1], scale=neg_top[:, t:t + 1])
+        z_b3 = tile([P, CHUNK, PACK], BF16, "z_b3")
+        nc.scalar.copy(z_b3[:], z_rows[:].rearrange("p t j -> p j t"))
+        z_c3 = tile([P, CHUNK], U32, "z_c3", "w2_raw")
+        z_s3 = tile([P, CHUNK], U8, "z_s3")
+        nc.vector.quantize_mx(out=z_c3[:].bitcast(FP8X4), scales=z_s3[:], in_=z_b3[:].rearrange("p j t -> p (j t)"))
+        z3 = (z_c3, z_s3)
+        kept = tile([P, 2 * CHUNK], F32, "kept", f"h{3 * CHUNK}")
+        nc.scalar.activation(kept[:], mom_g[:, 2 * CHUNK:], ACT.Copy, scale=drag_t[:])
+        scatter(2, *product(2, *z2))
+        scatter(3, *product(3, *z3))
 
         nc.sync.dma_start(out=out, in_=window[:])

@@ -17,13 +17,25 @@ ALU = mybir.AluOpType
 
 P = 128
 PACK = 4
-PASSES = K // (P * PACK)
+K_PASS = P * PACK
+PASSES = K // K_PASS
+QUADRANT = 32
+SCALE_ROWS = 4
+LIST_ROWS = 16
+PAIRS = 2
+PAIR = PACK // PAIRS
 HALF = 256
+HALVES = S // HALF
 CHUNK = 128
+CHUNKS = S // CHUNK
+LAST = CHUNKS - 1
+SCALAR_EMPTIES_FROM = 2
 KICK = 0.4
 
 
-def tile_picked_yham_drag_p_kernel(tc, x_words, x_scales, mom, w1, w2, bias, top, drag, offs, slot, out):
+def tile_picked_yham_drag_p_kernel(
+    tc, x_words, x_scales, mom, w1, w2, bias, top, drag, offs, slot, out
+):
     nc = tc.nc
     with ExitStack() as ctx:
         sb = ctx.enter_context(tc.tile_pool(name="sb", bufs=1))
@@ -32,11 +44,14 @@ def tile_picked_yham_drag_p_kernel(tc, x_words, x_scales, mom, w1, w2, bias, top
         def tile(shape, dtype, name, tag=None):
             return sb.tile(shape, dtype, name=name, tag=tag or name, align_bytes=64)
 
-        offs_t = sb.tile([P, S // 16], U16, name="offs_t")
-        slot_t = sb.tile([P, S // 16], U16, name="slot_t")
+        def entries(list_tile, first, count):
+            return list_tile[:, first // LIST_ROWS:(first + count) // LIST_ROWS]
+
+        offs_t = sb.tile([P, S // LIST_ROWS], U16, name="offs_t")
+        slot_t = sb.tile([P, S // LIST_ROWS], U16, name="slot_t")
         w1_raw = [tile([P, PACK, H], F32, f"w1_raw{g}") for g in range(PASSES)]
-        xw = [tile([P, T], U32, f"xw{g}") for g in range(PASSES)]
-        xs = tile([P, T], U8, "xs")
+        x_word_t = [tile([P, T], U32, f"xw{g}") for g in range(PASSES)]
+        x_scale_t = tile([P, T], U8, "xs")
         window = tile([P, U], F32, "window")
         w2_raw = tile([P, PACK, N], F32, "w2_raw")
         bias_t = tile([P, PACK], F32, "bias_t")
@@ -44,147 +59,140 @@ def tile_picked_yham_drag_p_kernel(tc, x_words, x_scales, mom, w1, w2, bias, top
         drag_t = tile([P, 1], F32, "drag_t")
 
         def load_w1(g):
-            nc.sync.dma_start(out=w1_raw[g][:], in_=w1[g * 512:(g + 1) * 512, :].rearrange("(p j) c -> p j c", j=PACK))
+            rows = w1[g * K_PASS:(g + 1) * K_PASS, :]
+            nc.sync.dma_start(out=w1_raw[g][:], in_=rows.rearrange("(p j) c -> p j c", j=PACK))
 
-        def load_x(g):
-            nc.sync.dma_start(out=xw[g][:].bitcast(I32), in_=x_words[g].rearrange("p n t -> p (n t)").bitcast(I32))
+        def load_x_words(g):
+            nc.sync.dma_start(out=x_word_t[g][:].bitcast(I32),
+                              in_=x_words[g].rearrange("p n j -> p (n j)").bitcast(I32))
 
-        def load_scales(engine):
-            for q in range(4):
-                engine.dma_start(out=xs[32 * q:32 * q + 4 * PASSES, :].bitcast(I32),
-                                 in_=x_scales[:, 4 * q:4 * q + 4, :].bitcast(I32))
-
-        def load_w2():
-            nc.sync.dma_start(out=w2_raw[:], in_=w2.rearrange("(p j) n -> p j n", j=PACK))
-
-        nc.vector.memset(xs[:].bitcast(I32), 0)
+        nc.vector.memset(x_scale_t[:].bitcast(I32), 0)
         load_w1(0)
-        load_scales(nc.sync)
+        for q in range(P // QUADRANT):
+            nc.sync.dma_start(out=x_scale_t[QUADRANT * q:QUADRANT * q + SCALE_ROWS * PASSES, :].bitcast(I32),
+                              in_=x_scales[:, SCALE_ROWS * q:SCALE_ROWS * (q + 1), :].bitcast(I32))
         nc.sync.dma_start(offs_t[:], offs)
         load_w1(1)
-        load_x(0)
+        load_x_words(0)
         nc.sync.dma_start(slot_t[:], slot)
-        load_x(1)
+        load_x_words(1)
         nc.sync.dma_start(out=bias_t[:], in_=bias.rearrange("(p t) o -> p (t o)", t=PACK))
         nc.sync.dma_start(out=top_t[:], in_=top.rearrange("(p t) o -> p (t o)", t=PACK))
         nc.sync.dma_start(out=drag_t[:], in_=drag)
         nc.sync.dma_start(out=window[:], in_=mom)
-        load_w2()
-
-        warm = tile([P, 1], F32, "warm")
-        warm_in = tile([P, 1], F32, "warm_in")
-        nc.vector.memset(warm_in[:], 0.0)
-        nc.scalar.activation(warm[:], warm_in[:], ACT.Tanh)
+        nc.sync.dma_start(out=w2_raw[:], in_=w2.rearrange("(p j) n -> p j n", j=PACK))
 
         neg_top = tile([P, PACK], F32, "neg_top")
         nc.gpsimd.tensor_scalar(neg_top[:], top_t[:], -1.0, 0.0, ALU.mult, ALU.add)
-        kick = tile([P, 1], F32, "kick")
-        nc.gpsimd.tensor_scalar(kick[:], drag_t[:], -KICK, 0.0, ALU.mult, ALU.add)
+        drag_kick = tile([P, 1], F32, "kick")
+        nc.gpsimd.tensor_scalar(drag_kick[:], drag_t[:], -KICK, 0.0, ALU.mult, ALU.add)
         drag_wide = tile([P, CHUNK], F32, "drag_wide")
         nc.gpsimd.tensor_scalar(drag_wide[:], drag_t[:].to_broadcast([P, CHUNK]), 1.0, 0.0, ALU.mult, ALU.add)
 
-        w1_c = [tile([P, H], U32, f"w1_c{g}") for g in range(PASSES)]
-        w1_s = [tile([P, H], U8, f"w1_s{g}") for g in range(PASSES)]
-        gs = tile([P, S], U8, "gs")
-
+        w1_codes = [tile([P, H], U32, f"w1_c{g}") for g in range(PASSES)]
+        w1_scales = [tile([P, H], U8, f"w1_s{g}") for g in range(PASSES)]
+        picked_scales = tile([P, S], U8, "gs")
         for g in range(PASSES):
-            src = w1_raw[g][:].rearrange("p j (m u t) -> p u m t j", u=2, t=2)
-            w1_b = [tile([P, 2 * P * PACK], BF16, f"w1_b{g}_{u}") for u in range(2)]
-            dst = [w1_b[u][:].rearrange("p (t m j) -> p m t j", t=2, j=PACK) for u in range(2)]
+            src = w1_raw[g][:].rearrange("p j (m u v) -> p u m v j", u=PAIRS, v=PAIR)
+            w1_bf = [tile([P, PAIR * P * PACK], BF16, f"w1_b{g}_{u}") for u in range(PAIRS)]
+            dst = [w1_bf[u][:].rearrange("p (v m j) -> p m v j", v=PAIR, j=PACK) for u in range(PAIRS)]
             nc.vector.tensor_copy(dst[0], src[:, 0])
             nc.scalar.copy(dst[1], src[:, 1])
             if g == 0:
-                nc.vector.tensor_copy(gs[:], xs[:].indirect(offs_t[:]))
-            for u in range(2):
-                cols = slice(u * 2 * P, (u + 1) * 2 * P)
-                nc.vector.quantize_mx(out=w1_c[g][:, cols].bitcast(FP8X4), scales=w1_s[g][:, cols], in_=w1_b[u][:])
+                nc.vector.tensor_copy(picked_scales[:], x_scale_t[:].indirect(offs_t[:]))
+            for u in range(PAIRS):
+                cols = slice(u * PAIR * P, (u + 1) * PAIR * P)
+                nc.vector.quantize_mx(out=w1_codes[g][:, cols].bitcast(FP8X4), scales=w1_scales[g][:, cols],
+                                      in_=w1_bf[u][:])
 
-        w2_b = tile([P, N * PACK], BF16, "w2_b")
-        w2_c = tile([P, N], U32, "w2_c")
-        w2_s = tile([P, N], U8, "w2_s")
+        w2_bf = tile([P, N * PACK], BF16, "w2_b")
+        w2_codes = tile([P, N], U32, "w2_c")
+        w2_scales = tile([P, N], U8, "w2_s")
 
-        def quantize_w2():
-            nc.vector.tensor_copy(w2_b[:].rearrange("p (n j) -> p n j", j=PACK), w2_raw[:].rearrange("p j n -> p n j"))
-            nc.vector.quantize_mx(out=w2_c[:].bitcast(FP8X4), scales=w2_s[:], in_=w2_b[:])
-
-        halves = S // HALF
-        gx = [[tile([P, HALF], U32, f"gx{g}_{a}") for a in range(halves)] for g in range(PASSES)]
-        banks = [[ps.tile([P, HALF], F32, name=f"pre{a}_{t}", tag=f"bank{a}_{t}") for t in range(PACK)] for a in range(halves)]
+        picked_words = [[tile([P, HALF], U32, f"gx{g}_{a}") for a in range(HALVES)] for g in range(PASSES)]
+        pre = [[ps.tile([P, HALF], F32, name=f"pre{a}_{t}", tag=f"bank{a}_{t}") for t in range(PACK)]
+               for a in range(HALVES)]
         for g in range(PASSES):
-            for a in range(halves):
-                nc.vector.tensor_copy(gx[g][a][:], xw[g][:].indirect(offs_t[:, a * HALF // 16:(a + 1) * HALF // 16]))
+            for a in range(HALVES):
+                nc.vector.tensor_copy(picked_words[g][a][:], x_word_t[g][:].indirect(entries(offs_t, a * HALF, HALF)))
                 for t in range(PACK):
                     nc.tensor.matmul_mx(
-                        out=banks[a][t][:],
-                        lhsT=w1_c[g][:, t * P:(t + 1) * P].bitcast(FP8X4),
-                        lhsT_scale=w1_s[g][:, t * P:(t + 1) * P],
-                        rhs=gx[g][a][:].bitcast(FP8X4),
-                        rhs_scale=gs[4 * g:P, a * HALF:(a + 1) * HALF],
+                        out=pre[a][t][:],
+                        lhsT=w1_codes[g][:, t * P:(t + 1) * P].bitcast(FP8X4),
+                        lhsT_scale=w1_scales[g][:, t * P:(t + 1) * P],
+                        rhs=picked_words[g][a][:].bitcast(FP8X4),
+                        rhs_scale=picked_scales[SCALE_ROWS * g:P, a * HALF:(a + 1) * HALF],
                         start=(g == 0), stop=(g == PASSES - 1))
 
-        mom_g = tile([P, S], F32, "mom_g")
-        nc.vector.tensor_copy(mom_g[:], window[:].indirect(slot_t[:]))
-        quantize_w2()
+        mom_picked = tile([P, S], F32, "mom_g")
+        nc.vector.tensor_copy(mom_picked[:], window[:].indirect(slot_t[:]))
+        nc.vector.tensor_copy(w2_bf[:].rearrange("p (n j) -> p n j", j=PACK), w2_raw[:].rearrange("p j n -> p n j"))
+        nc.vector.quantize_mx(out=w2_codes[:].bitcast(FP8X4), scales=w2_scales[:], in_=w2_bf[:])
 
-
-        def tanh_run(start, size):
-            a, b = divmod(start, HALF)
-            h = tile([P, PACK, size], F32, f"h{start}")
+        def tanh_chunk(c):
+            a, first = divmod(c * CHUNK, HALF)
+            h = tile([P, PACK, CHUNK], F32, f"h{c}")
             for t in range(PACK):
-                nc.scalar.activation(h[:, t, :], banks[a][t][:, b:b + size], ACT.Tanh, bias=bias_t[:, t:t + 1])
+                nc.scalar.activation(h[:, t, :], pre[a][t][:, first:first + CHUNK], ACT.Tanh, bias=bias_t[:, t:t + 1])
             return h
 
-        def hidden(start, size, h):
-            hh = tile([P, size, PACK], F32, f"hh{start}")
-            z_b = tile([P, size, PACK], BF16, f"z_b{start}", "w2_raw")
-            z_c = tile([P, size], U32, f"z_c{start}")
-            z_s = tile([P, size], U8, f"z_s{start}")
-            nc.scalar.activation(hh[:], h.rearrange("p t j -> p j t"), ACT.Square)
-            nc.vector.scalar_tensor_tensor(z_b[:], hh[:], 1.0,
-                                           neg_top[:].unsqueeze(1).to_broadcast([P, size, PACK]),
+        def quantize_z(z_bf, z_codes, z_scales):
+            nc.vector.quantize_mx(out=z_codes[:].bitcast(FP8X4), scales=z_scales[:],
+                                  in_=z_bf[:].rearrange("p j t -> p (j t)"))
+            return z_codes, z_scales
+
+        def z_shared(c):
+            h = tanh_chunk(c)
+            hh = tile([P, CHUNK, PACK], F32, f"hh{c}")
+            z_bf = tile([P, CHUNK, PACK], BF16, f"z_b{c}", "w2_raw")
+            z_codes = tile([P, CHUNK], U32, f"z_c{c}")
+            z_scales = tile([P, CHUNK], U8, f"z_s{c}")
+            nc.scalar.activation(hh[:], h[:].rearrange("p t j -> p j t"), ACT.Square)
+            nc.vector.scalar_tensor_tensor(z_bf[:], hh[:], 1.0, neg_top[:].unsqueeze(1).to_broadcast([P, CHUNK, PACK]),
                                            ALU.subtract, ALU.mult)
-            nc.vector.quantize_mx(out=z_c[:].bitcast(FP8X4), scales=z_s[:], in_=z_b[:].rearrange("p j t -> p (j t)"))
-            return z_c, z_s
+            return quantize_z(z_bf, z_codes, z_scales)
 
-        def product(c, z_c, z_s):
+        def z_on_scalar(c):
+            h = tanh_chunk(c)
+            hh = tile([P, PACK, CHUNK], F32, f"hh{c}")
+            nc.scalar.activation(hh[:], h[:], ACT.Square)
+            z_groups = tile([P, PACK, CHUNK], BF16, "z_rows")
+            for t in range(PACK):
+                nc.scalar.activation(z_groups[:, t, :], hh[:, t, :], ACT.Identity,
+                                     bias=top_t[:, t:t + 1], scale=neg_top[:, t:t + 1])
+            z_bf = tile([P, CHUNK, PACK], BF16, f"z_b{c}")
+            nc.scalar.copy(z_bf[:], z_groups[:].rearrange("p t j -> p j t"))
+            z_codes = tile([P, CHUNK], U32, f"z_c{c}", "w2_raw")
+            z_scales = tile([P, CHUNK], U8, f"z_s{c}")
+            return quantize_z(z_bf, z_codes, z_scales)
+
+        def second_product(c, z_codes, z_scales):
             y = ps.tile([P, CHUNK], F32, name=f"y{c}", tag=f"bank0_{c}")
-            nc.tensor.matmul_mx(out=y[:], lhsT=w2_c[:].bitcast(FP8X4), lhsT_scale=w2_s[:],
-                                rhs=z_c[:].bitcast(FP8X4), rhs_scale=z_s[:], start=True, stop=True)
-            if c < 2:
-                p = tile([P, CHUNK], F32, f"p{c}", f"h{(c + 1) * CHUNK}")
-                nc.vector.scalar_tensor_tensor(p[:], y[:], -KICK, mom_g[:, c * CHUNK:(c + 1) * CHUNK], ALU.mult, ALU.add)
-                return p[:], drag_wide[:], ALU.mult
+            nc.tensor.matmul_mx(out=y[:], lhsT=w2_codes[:].bitcast(FP8X4), lhsT_scale=w2_scales[:],
+                                rhs=z_codes[:].bitcast(FP8X4), rhs_scale=z_scales[:], start=True, stop=True)
+            return y
+
+        def put_from_vector(c, z):
+            y = second_product(c, *z)
+            p = tile([P, CHUNK], F32, f"p{c}", f"h{c + 1}")
+            nc.vector.scalar_tensor_tensor(p[:], y[:], -KICK, mom_picked[:, c * CHUNK:(c + 1) * CHUNK],
+                                           ALU.mult, ALU.add)
+            nc.vector.tensor_tensor(window[:].indirect(entries(slot_t, c * CHUNK, CHUNK)), p[:], drag_wide[:], ALU.mult)
+
+        def put_from_scalar(c, z, kept):
+            y = second_product(c, *z)
             kicked = tile([P, CHUNK], F32, f"kicked{c}")
-            nc.scalar.activation(kicked[:], y[:], ACT.Copy, scale=kick[:])
-            return kept[:, (c - 2) * CHUNK:(c - 1) * CHUNK], kicked[:], ALU.add
+            nc.scalar.activation(kicked[:], y[:], ACT.Copy, scale=drag_kick[:])
+            nc.vector.tensor_tensor(window[:].indirect(entries(slot_t, c * CHUNK, CHUNK)), kept, kicked[:], ALU.add)
 
-        def scatter(c, in0, in1, op):
-            nc.vector.tensor_tensor(window[:].indirect(slot_t[:, c * CHUNK // 16:(c + 1) * CHUNK // 16]), in0, in1, op)
-
-        def make_z(c):
-            return hidden(c * CHUNK, CHUNK, tanh_run(c * CHUNK, CHUNK)[:])
-
-        z0 = make_z(0)
-        z1 = make_z(1)
-        scatter(0, *product(0, *z0))
-        z2 = make_z(2)
-        r1 = product(1, *z1)
-        scatter(1, *r1)
-        h3 = tanh_run(3 * CHUNK, CHUNK)
-        hh3 = tile([P, PACK, CHUNK], F32, "hh3")
-        nc.scalar.activation(hh3[:], h3[:], ACT.Square)
-        z_rows = tile([P, PACK, CHUNK], BF16, "z_rows")
-        for t in range(PACK):
-            nc.scalar.activation(z_rows[:, t, :], hh3[:, t, :], ACT.Identity, bias=top_t[:, t:t + 1], scale=neg_top[:, t:t + 1])
-        z_b3 = tile([P, CHUNK, PACK], BF16, "z_b3")
-        nc.scalar.copy(z_b3[:], z_rows[:].rearrange("p t j -> p j t"))
-        z_c3 = tile([P, CHUNK], U32, "z_c3", "w2_raw")
-        z_s3 = tile([P, CHUNK], U8, "z_s3")
-        nc.vector.quantize_mx(out=z_c3[:].bitcast(FP8X4), scales=z_s3[:], in_=z_b3[:].rearrange("p j t -> p (j t)"))
-        z3 = (z_c3, z_s3)
-        kept = tile([P, 2 * CHUNK], F32, "kept", f"h{3 * CHUNK}")
-        nc.scalar.activation(kept[:], mom_g[:, 2 * CHUNK:], ACT.Copy, scale=drag_t[:])
-        scatter(2, *product(2, *z2))
-        scatter(3, *product(3, *z3))
+        z = [z_shared(0)]
+        for c in range(1, LAST):
+            z.append(z_shared(c))
+            put_from_vector(c - 1, z[c - 1])
+        z.append(z_on_scalar(LAST))
+        kept_all = tile([P, S - SCALAR_EMPTIES_FROM * CHUNK], F32, "kept", f"h{LAST}")
+        nc.scalar.activation(kept_all[:], mom_picked[:, SCALAR_EMPTIES_FROM * CHUNK:], ACT.Copy, scale=drag_t[:])
+        for i, c in enumerate(range(SCALAR_EMPTIES_FROM, CHUNKS)):
+            put_from_scalar(c, z[c], kept_all[:, i * CHUNK:(i + 1) * CHUNK])
 
         nc.sync.dma_start(out=out, in_=window[:])

@@ -30,6 +30,7 @@ CHUNK = 128
 CHUNKS = S // CHUNK
 LAST = CHUNKS - 1
 SCALAR_EMPTIES_FROM = 2
+W2_AT = 12928
 KICK = 0.4
 
 
@@ -40,6 +41,10 @@ def tile_picked_yham_drag_p_kernel(
     with ExitStack() as ctx:
         sb = ctx.enter_context(tc.tile_pool(name="sb", bufs=1))
         ps = ctx.enter_context(tc.psum_pool(name="ps", bufs=1))
+        laid = ctx.enter_context(tc.tile_pool(name="laid", bufs=1))
+
+        def placed(shape, dtype, name, offset, tag=None):
+            return laid.tile(shape, dtype, name=name, tag=tag or name, align_bytes=64, offset=offset)
 
         def tile(shape, dtype, name, tag=None):
             return sb.tile(shape, dtype, name=name, tag=tag or name, align_bytes=64)
@@ -50,13 +55,15 @@ def tile_picked_yham_drag_p_kernel(
         offs_t = sb.tile([P, S // LIST_ROWS], U16, name="offs_t")
         slot_t = sb.tile([P, S // LIST_ROWS], U16, name="slot_t")
         w1_raw = [tile([P, PACK, H], F32, f"w1_raw{g}") for g in range(PASSES)]
-        x_word_t = [tile([P, T], U32, f"xw{g}") for g in range(PASSES)]
-        x_scale_t = tile([P, T], U8, "xs")
-        window = tile([P, U], F32, "window")
-        w2_raw = tile([P, PACK, N], F32, "w2_raw")
-        bias_t = tile([P, PACK], F32, "bias_t")
-        top_t = tile([P, PACK], F32, "top_t")
-        drag_t = tile([P, 1], F32, "drag_t")
+        x_word_t = [tile([P, T], U32, "xw0"), placed([P, T], U32, "xw1", 0)]
+        x_scale_t = placed([P, T], U8, "xs", 8128)
+        bias_t = placed([P, PACK], F32, "bias_t", 8192)
+        top_t = placed([P, PACK], F32, "top_t", 8256)
+        drag_t = placed([P, 1], F32, "drag_t", 8320)
+        window = placed([P, U], F32, "window", 8384)
+        picked_rows = placed([P, S], U8, "picked_rows", 12480)
+        w2_raw = placed([P, PACK, N], F32, "w2_raw", W2_AT)
+        picked_scales = tile([P, PASSES, S], U8, "gs")
 
         def load_w1(g):
             rows = w1[g * K_PASS:(g + 1) * K_PASS, :]
@@ -67,14 +74,18 @@ def tile_picked_yham_drag_p_kernel(
                               in_=x_words[g].rearrange("p n j -> p (n j)").bitcast(I32))
 
         nc.vector.memset(x_scale_t[:].bitcast(I32), 0)
-        load_w1(0)
-        for q in range(P // QUADRANT):
-            nc.sync.dma_start(out=x_scale_t[QUADRANT * q:QUADRANT * q + SCALE_ROWS * PASSES, :].bitcast(I32),
-                              in_=x_scales[:, SCALE_ROWS * q:SCALE_ROWS * (q + 1), :].bitcast(I32))
+        nc.vector.memset(picked_scales[:].rearrange("p g s -> p (g s)").bitcast(I32), 0)
         nc.sync.dma_start(offs_t[:], offs)
+        load_w1(0)
+        nc.sync.dma_start(out=x_scale_t[0:P:SCALE_ROWS, :].bitcast(I32),
+                          in_=x_scales.rearrange("g b n -> b g n").bitcast(I32))
         load_w1(1)
         load_x_words(0)
         nc.sync.dma_start(slot_t[:], slot)
+        nc.vector.tensor_copy(picked_rows[:], x_scale_t[:].indirect(offs_t[:]))
+        for q in range(P // QUADRANT):
+            nc.sync.dma_start(out=picked_scales[QUADRANT * q:QUADRANT * q + SCALE_ROWS, :, :].bitcast(I32),
+                              in_=picked_rows[QUADRANT * q:QUADRANT * (q + 1):SCALE_ROWS, :].bitcast(I32))
         load_x_words(1)
         nc.sync.dma_start(out=bias_t[:], in_=bias.rearrange("(p t) o -> p (t o)", t=PACK))
         nc.sync.dma_start(out=top_t[:], in_=top.rearrange("(p t) o -> p (t o)", t=PACK))
@@ -91,15 +102,12 @@ def tile_picked_yham_drag_p_kernel(
 
         w1_codes = [tile([P, H], U32, f"w1_c{g}") for g in range(PASSES)]
         w1_scales = [tile([P, H], U8, f"w1_s{g}") for g in range(PASSES)]
-        picked_scales = tile([P, S], U8, "gs")
         for g in range(PASSES):
             src = w1_raw[g][:].rearrange("p j (m u v) -> p u m v j", u=PAIRS, v=PAIR)
             w1_bf = [tile([P, PAIR * P * PACK], BF16, f"w1_b{g}_{u}") for u in range(PAIRS)]
             dst = [w1_bf[u][:].rearrange("p (v m j) -> p m v j", v=PAIR, j=PACK) for u in range(PAIRS)]
             nc.vector.tensor_copy(dst[0], src[:, 0])
             nc.scalar.copy(dst[1], src[:, 1])
-            if g == 0:
-                nc.vector.tensor_copy(picked_scales[:], x_scale_t[:].indirect(offs_t[:]))
             for u in range(PAIRS):
                 cols = slice(u * PAIR * P, (u + 1) * PAIR * P)
                 nc.vector.quantize_mx(out=w1_codes[g][:, cols].bitcast(FP8X4), scales=w1_scales[g][:, cols],
@@ -121,7 +129,7 @@ def tile_picked_yham_drag_p_kernel(
                         lhsT=w1_codes[g][:, t * P:(t + 1) * P].bitcast(FP8X4),
                         lhsT_scale=w1_scales[g][:, t * P:(t + 1) * P],
                         rhs=picked_words[g][a][:].bitcast(FP8X4),
-                        rhs_scale=picked_scales[SCALE_ROWS * g:P, a * HALF:(a + 1) * HALF],
+                        rhs_scale=picked_scales[:, g, a * HALF:(a + 1) * HALF],
                         start=(g == 0), stop=(g == PASSES - 1))
 
         mom_picked = tile([P, S], F32, "mom_g")
@@ -144,7 +152,7 @@ def tile_picked_yham_drag_p_kernel(
         def z_shared(c):
             h = tanh_chunk(c)
             hh = tile([P, CHUNK, PACK], F32, f"hh{c}")
-            z_bf = tile([P, CHUNK, PACK], BF16, f"z_b{c}", "w2_raw")
+            z_bf = placed([P, CHUNK, PACK], BF16, f"z_b{c}", W2_AT, "w2_raw")
             z_codes = tile([P, CHUNK], U32, f"z_c{c}")
             z_scales = tile([P, CHUNK], U8, f"z_s{c}")
             nc.scalar.activation(hh[:], h[:].rearrange("p t j -> p j t"), ACT.Square)
@@ -162,7 +170,7 @@ def tile_picked_yham_drag_p_kernel(
                                      bias=top_t[:, t:t + 1], scale=neg_top[:, t:t + 1])
             z_bf = tile([P, CHUNK, PACK], BF16, f"z_b{c}")
             nc.scalar.copy(z_bf[:], z_groups[:].rearrange("p t j -> p j t"))
-            z_codes = tile([P, CHUNK], U32, f"z_c{c}", "w2_raw")
+            z_codes = placed([P, CHUNK], U32, f"z_c{c}", W2_AT, "w2_raw")
             z_scales = tile([P, CHUNK], U8, f"z_s{c}")
             return quantize_z(z_bf, z_codes, z_scales)
 

@@ -30,7 +30,7 @@ CHUNK = 128
 CHUNKS = S // CHUNK
 LAST = CHUNKS - 1
 SCALAR_EMPTIES_FROM = 2
-W2_AT = 12928
+W2_AT = 15168
 KICK = 0.4
 
 
@@ -56,12 +56,12 @@ def tile_picked_yham_drag_p_kernel(
         slot_t = sb.tile([P, S // LIST_ROWS], U16, name="slot_t")
         w1_raw = [tile([P, PACK, H], F32, f"w1_raw{g}") for g in range(PASSES)]
         x_word_t = [tile([P, T], U32, "xw0"), placed([P, T], U32, "xw1", 0)]
-        x_scale_t = placed([P, T], U8, "xs", 8128)
+        x_scale_t = placed([P, T + 512], U8, "xs", 8128)
         bias_t = placed([P, PACK], F32, "bias_t", 8192)
         top_t = placed([P, PACK], F32, "top_t", 8256)
-        drag_t = placed([P, 1], F32, "drag_t", 8320)
-        window = placed([P, U], F32, "window", 8384)
-        picked_rows = placed([P, S], U8, "picked_rows", 12480)
+        drag_t = tile([P, 1], F32, "drag_t")
+        window = placed([P, U], F32, "window", 10624)
+        picked_rows = placed([P, S], U8, "picked_rows", 14720)
         w2_raw = placed([P, PACK, N], F32, "w2_raw", W2_AT)
         picked_scales = tile([P, PASSES, S], U8, "gs")
 
@@ -73,38 +73,39 @@ def tile_picked_yham_drag_p_kernel(
             nc.sync.dma_start(out=x_word_t[g][:].bitcast(I32),
                               in_=x_words[g].rearrange("p n j -> p (n j)").bitcast(I32))
 
-        nc.vector.memset(x_scale_t[:].bitcast(I32), 0)
+        nc.vector.memset(x_scale_t[:, 0:T].bitcast(I32), 0)
         nc.vector.memset(picked_scales[:].rearrange("p g s -> p (g s)").bitcast(I32), 0)
-        nc.sync.dma_start(offs_t[:], offs)
         load_w1(0)
-        nc.sync.dma_start(out=x_scale_t[0:P:SCALE_ROWS, :].bitcast(I32),
+        nc.sync.dma_start(offs_t[:], offs)
+        nc.sync.dma_start(out=x_scale_t[0:P:SCALE_ROWS, 0:T].bitcast(I32),
                           in_=x_scales.rearrange("g b n -> b g n").bitcast(I32))
-        load_w1(1)
         load_x_words(0)
+        load_w1(1)
         nc.sync.dma_start(slot_t[:], slot)
-        nc.vector.tensor_copy(picked_rows[:], x_scale_t[:].indirect(offs_t[:]))
+        nc.sync.dma_start(out=drag_t[:], in_=drag)
+        nc.vector.tensor_copy(picked_rows[:], x_scale_t[:, 0:T].indirect(offs_t[:]))
         for q in range(P // QUADRANT):
             nc.sync.dma_start(out=picked_scales[QUADRANT * q:QUADRANT * q + SCALE_ROWS, :, :].bitcast(I32),
                               in_=picked_rows[QUADRANT * q:QUADRANT * (q + 1):SCALE_ROWS, :].bitcast(I32))
         load_x_words(1)
         nc.sync.dma_start(out=bias_t[:], in_=bias.rearrange("(p t) o -> p (t o)", t=PACK))
-        nc.sync.dma_start(out=top_t[:], in_=top.rearrange("(p t) o -> p (t o)", t=PACK))
-        nc.sync.dma_start(out=drag_t[:], in_=drag)
         nc.sync.dma_start(out=window[:], in_=mom)
+        nc.sync.dma_start(out=top_t[:], in_=top.rearrange("(p t) o -> p (t o)", t=PACK))
         nc.sync.dma_start(out=w2_raw[:], in_=w2.rearrange("(p j) n -> p j n", j=PACK))
 
         neg_top = tile([P, PACK], F32, "neg_top")
-        nc.gpsimd.tensor_scalar(neg_top[:], top_t[:], -1.0, 0.0, ALU.mult, ALU.add)
+        nc.scalar.activation(neg_top[:], top_t[:], ACT.Copy, scale=-1.0)
         drag_kick = tile([P, 1], F32, "kick")
-        nc.gpsimd.tensor_scalar(drag_kick[:], drag_t[:], -KICK, 0.0, ALU.mult, ALU.add)
+        nc.vector.tensor_scalar(drag_kick[:], drag_t[:], KICK, 0.0, ALU.mult, ALU.add)
         drag_wide = tile([P, CHUNK], F32, "drag_wide")
-        nc.gpsimd.tensor_scalar(drag_wide[:], drag_t[:].to_broadcast([P, CHUNK]), 1.0, 0.0, ALU.mult, ALU.add)
+        nc.vector.tensor_scalar(drag_wide[:], drag_t[:].to_broadcast([P, CHUNK]), 1.0, 0.0, ALU.mult, ALU.add)
 
         w1_codes = [tile([P, H], U32, f"w1_c{g}") for g in range(PASSES)]
         w1_scales = [tile([P, H], U8, f"w1_s{g}") for g in range(PASSES)]
         for g in range(PASSES):
             src = w1_raw[g][:].rearrange("p j (m u v) -> p u m v j", u=PAIRS, v=PAIR)
-            w1_bf = [tile([P, PAIR * P * PACK], BF16, f"w1_b{g}_{u}") for u in range(PAIRS)]
+            w1_bf = [placed([P, PAIR * P * PACK], BF16, "w1_first", 8320) if g == 0 and u == 0
+                     else tile([P, PAIR * P * PACK], BF16, f"w1_b{g}_{u}") for u in range(PAIRS)]
             dst = [w1_bf[u][:].rearrange("p (v m j) -> p m v j", v=PAIR, j=PACK) for u in range(PAIRS)]
             nc.vector.tensor_copy(dst[0], src[:, 0])
             nc.scalar.copy(dst[1], src[:, 1])
@@ -155,8 +156,9 @@ def tile_picked_yham_drag_p_kernel(
             z_bf = placed([P, CHUNK, PACK], BF16, f"z_b{c}", W2_AT, "w2_raw")
             z_codes = tile([P, CHUNK], U32, f"z_c{c}")
             z_scales = tile([P, CHUNK], U8, f"z_s{c}")
-            nc.scalar.activation(hh[:], h[:].rearrange("p t j -> p j t"), ACT.Square)
-            nc.vector.scalar_tensor_tensor(z_bf[:], hh[:], 1.0, neg_top[:].unsqueeze(1).to_broadcast([P, CHUNK, PACK]),
+            nc.scalar.activation(hh[:].rearrange("p (c i) t -> p c t i", i=4),
+                                 h[:].rearrange("p t (c i) -> p c t i", i=4), ACT.Square)
+            nc.vector.scalar_tensor_tensor(z_bf[:], hh[:], 1.0, top_t[:].unsqueeze(1).to_broadcast([P, CHUNK, PACK]),
                                            ALU.subtract, ALU.mult)
             return quantize_z(z_bf, z_codes, z_scales)
 
@@ -167,9 +169,9 @@ def tile_picked_yham_drag_p_kernel(
             z_groups = tile([P, PACK, CHUNK], BF16, "z_rows")
             for t in range(PACK):
                 nc.scalar.activation(z_groups[:, t, :], hh[:, t, :], ACT.Identity,
-                                     bias=top_t[:, t:t + 1], scale=neg_top[:, t:t + 1])
+                                     bias=neg_top[:, t:t + 1], scale=top_t[:, t:t + 1])
             z_bf = tile([P, CHUNK, PACK], BF16, f"z_b{c}")
-            nc.scalar.copy(z_bf[:], z_groups[:].rearrange("p t j -> p j t"))
+            nc.scalar.copy(z_bf[:].rearrange("p (c i) t -> p c t i", i=4), z_groups[:].rearrange("p t (c i) -> p c t i", i=4))
             z_codes = placed([P, CHUNK], U32, f"z_c{c}", W2_AT, "w2_raw")
             z_scales = tile([P, CHUNK], U8, f"z_s{c}")
             return quantize_z(z_bf, z_codes, z_scales)
@@ -183,9 +185,10 @@ def tile_picked_yham_drag_p_kernel(
         def put_from_vector(c, z):
             y = second_product(c, *z)
             p = tile([P, CHUNK], F32, f"p{c}", f"h{c + 1}")
-            nc.vector.scalar_tensor_tensor(p[:], y[:], -KICK, mom_picked[:, c * CHUNK:(c + 1) * CHUNK],
+            nc.vector.scalar_tensor_tensor(p[:], y[:], KICK, mom_picked[:, c * CHUNK:(c + 1) * CHUNK],
                                            ALU.mult, ALU.add)
-            nc.vector.tensor_tensor(window[:].indirect(entries(slot_t, c * CHUNK, CHUNK)), p[:], drag_wide[:], ALU.mult)
+            nc.vector.tensor_tensor(window[:].indirect(entries(slot_t, c * CHUNK, CHUNK)), p[:], drag_wide[:],
+                                    ALU.mult)
 
         def put_from_scalar(c, z, kept):
             y = second_product(c, *z)

@@ -135,11 +135,20 @@ def tile_picked_yham_drag_p_kernel(
 
         mom_picked = tile([P, S], F32, "mom_g")
         nc.vector.tensor_copy(mom_picked[:], window[:].indirect(slot_t[:]))
-        nc.vector.tensor_copy(w2_bf[:].rearrange("p (n j) -> p n j", j=PACK), w2_raw[:].rearrange("p j n -> p n j"))
+        nc.vector.tensor_copy(w2_bf[:].rearrange("p (c i j) -> p c j i", i=4, j=PACK),
+                              w2_raw[:].rearrange("p j (c i) -> p c j i", i=4))
         nc.vector.quantize_mx(out=w2_codes[:].bitcast(FP8X4), scales=w2_scales[:], in_=w2_bf[:])
+
+        wide = []
 
         def tanh_chunk(c):
             a, first = divmod(c * CHUNK, HALF)
+            if c == 2:
+                wide.append(tile([P, PACK, HALF], F32, "h2"))
+                for t in range(PACK):
+                    nc.scalar.activation(wide[0][:, t, :], pre[a][t][:], ACT.Tanh, bias=bias_t[:, t:t + 1])
+            if c >= 2:
+                return wide[0][:, :, first:first + CHUNK]
             h = tile([P, PACK, CHUNK], F32, f"h{c}")
             for t in range(PACK):
                 nc.scalar.activation(h[:, t, :], pre[a][t][:, first:first + CHUNK], ACT.Tanh, bias=bias_t[:, t:t + 1])
@@ -153,7 +162,8 @@ def tile_picked_yham_drag_p_kernel(
         def z_shared(c):
             h = tanh_chunk(c)
             hh = tile([P, CHUNK, PACK], F32, f"hh{c}")
-            z_bf = placed([P, CHUNK, PACK], BF16, f"z_b{c}", W2_AT, "w2_raw")
+            z_bf = (placed([P, CHUNK, PACK], BF16, "z_b0", W2_AT, "w2_raw") if c == 0
+                    else tile([P, CHUNK, PACK], BF16, f"z_b{c}", "hh0"))
             z_codes = tile([P, CHUNK], U32, f"z_c{c}")
             z_scales = tile([P, CHUNK], U8, f"z_s{c}")
             nc.scalar.activation(hh[:].rearrange("p (c i) t -> p c t i", i=4),
@@ -172,7 +182,7 @@ def tile_picked_yham_drag_p_kernel(
                                      bias=neg_top[:, t:t + 1], scale=top_t[:, t:t + 1])
             z_bf = tile([P, CHUNK, PACK], BF16, f"z_b{c}")
             nc.scalar.copy(z_bf[:].rearrange("p (c i) t -> p c t i", i=4), z_groups[:].rearrange("p t (c i) -> p c t i", i=4))
-            z_codes = placed([P, CHUNK], U32, f"z_c{c}", W2_AT, "w2_raw")
+            z_codes = tile([P, CHUNK], U32, f"z_c{c}", "hh0")
             z_scales = tile([P, CHUNK], U8, f"z_s{c}")
             return quantize_z(z_bf, z_codes, z_scales)
 
@@ -184,7 +194,7 @@ def tile_picked_yham_drag_p_kernel(
 
         def put_from_vector(c, z):
             y = second_product(c, *z)
-            p = tile([P, CHUNK], F32, f"p{c}", f"h{c + 1}")
+            p = tile([P, CHUNK], F32, f"p{c}", "h1" if c == 0 else "hh1")
             nc.vector.scalar_tensor_tensor(p[:], y[:], KICK, mom_picked[:, c * CHUNK:(c + 1) * CHUNK],
                                            ALU.mult, ALU.add)
             nc.vector.tensor_tensor(window[:].indirect(entries(slot_t, c * CHUNK, CHUNK)), p[:], drag_wide[:],
@@ -201,7 +211,7 @@ def tile_picked_yham_drag_p_kernel(
             z.append(z_shared(c))
             put_from_vector(c - 1, z[c - 1])
         z.append(z_on_scalar(LAST))
-        kept_all = tile([P, S - SCALAR_EMPTIES_FROM * CHUNK], F32, "kept", f"h{LAST}")
+        kept_all = tile([P, S - SCALAR_EMPTIES_FROM * CHUNK], F32, "kept", "h2")
         nc.scalar.activation(kept_all[:], mom_picked[:, SCALAR_EMPTIES_FROM * CHUNK:], ACT.Copy, scale=drag_t[:])
         for i, c in enumerate(range(SCALAR_EMPTIES_FROM, CHUNKS)):
             put_from_scalar(c, z[c], kept_all[:, i * CHUNK:(i + 1) * CHUNK])

@@ -140,6 +140,7 @@ def tile_picked_yham_drag_p_kernel(
         nc.vector.quantize_mx(out=w2_codes[:].bitcast(FP8X4), scales=w2_scales[:], in_=w2_bf[:])
 
         wide = []
+        kept_list = []
 
         def tanh_chunk(c):
             a, first = divmod(c * CHUNK, HALF)
@@ -159,8 +160,16 @@ def tile_picked_yham_drag_p_kernel(
                                   in_=z_bf[:].rearrange("p j t -> p (j t)"))
             return z_codes, z_scales
 
+        hh_last = tile([P, PACK, CHUNK], F32, "hh_last")
+
+        def square_last(u):
+            groups = slice(u * PAIR, (u + 1) * PAIR)
+            nc.scalar.activation(hh_last[:, groups, :], wide[0][:, groups, CHUNK:HALF], ACT.Square)
+
         def z_shared(c):
             h = tanh_chunk(c)
+            if c == 2:
+                square_last(0)
             hh = tile([P, CHUNK, PACK], F32, f"hh{c}")
             z_bf = (placed([P, CHUNK, PACK], BF16, "z_b0", W2_AT, "w2_raw") if c == 0
                     else tile([P, CHUNK, PACK], BF16, f"z_b{c}", "hh0"))
@@ -173,13 +182,15 @@ def tile_picked_yham_drag_p_kernel(
             return quantize_z(z_bf, z_codes, z_scales)
 
         def z_on_scalar(c):
-            h = tanh_chunk(c)
-            hh = tile([P, PACK, CHUNK], F32, f"hh{c}")
-            nc.scalar.activation(hh[:], h[:], ACT.Square)
+            hh = hh_last
+            square_last(1)
             z_groups = tile([P, PACK, CHUNK], BF16, "z_rows")
             for t in range(PACK):
                 nc.scalar.activation(z_groups[:, t, :], hh[:, t, :], ACT.Identity,
                                      bias=neg_top[:, t:t + 1], scale=top_t[:, t:t + 1])
+            kept_all = tile([P, S - SCALAR_EMPTIES_FROM * CHUNK], F32, "kept", "h2")
+            nc.scalar.activation(kept_all[:], mom_picked[:, SCALAR_EMPTIES_FROM * CHUNK:], ACT.Copy, scale=drag_t[:])
+            kept_list.append(kept_all)
             z_bf = tile([P, CHUNK, PACK], BF16, f"z_b{c}")
             nc.scalar.copy(z_bf[:].rearrange("p (c i) t -> p c t i", i=4), z_groups[:].rearrange("p t (c i) -> p c t i", i=4))
             z_codes = tile([P, CHUNK], U32, f"z_c{c}", "hh0")
@@ -202,7 +213,7 @@ def tile_picked_yham_drag_p_kernel(
 
         def put_from_scalar(c, z, kept):
             y = second_product(c, *z)
-            kicked = tile([P, CHUNK], F32, f"kicked{c}")
+            kicked = tile([P, CHUNK], F32, f"kicked{c}", "hh_last" if c < LAST else None)
             nc.scalar.activation(kicked[:], y[:], ACT.Copy, scale=drag_kick[:])
             nc.vector.tensor_tensor(window[:].indirect(entries(slot_t, c * CHUNK, CHUNK)), kept, kicked[:], ALU.add)
 
@@ -211,8 +222,7 @@ def tile_picked_yham_drag_p_kernel(
             z.append(z_shared(c))
             put_from_vector(c - 1, z[c - 1])
         z.append(z_on_scalar(LAST))
-        kept_all = tile([P, S - SCALAR_EMPTIES_FROM * CHUNK], F32, "kept", "h2")
-        nc.scalar.activation(kept_all[:], mom_picked[:, SCALAR_EMPTIES_FROM * CHUNK:], ACT.Copy, scale=drag_t[:])
+        kept_all = kept_list[0]
         for i, c in enumerate(range(SCALAR_EMPTIES_FROM, CHUNKS)):
             put_from_scalar(c, z[c], kept_all[:, i * CHUNK:(i + 1) * CHUNK])
 

@@ -59,7 +59,7 @@ def tile_picked_yham_drag_p_kernel(
         x_scale_t = placed([P, T + 512], U8, "xs", 8128)
         bias_t = placed([P, PACK], F32, "bias_t", 8192)
         top_t = placed([P, PACK], F32, "top_t", 8256)
-        drag_t = tile([P, 1], F32, "drag_t")
+        drag_t = placed([P, 1], F32, "drag_t", 10432)
         window = placed([P, U], F32, "window", 10624)
         picked_rows = placed([P, S], U8, "picked_rows", 14720)
         w2_raw = placed([P, PACK, N], F32, "w2_raw", W2_AT)
@@ -81,22 +81,22 @@ def tile_picked_yham_drag_p_kernel(
                           in_=x_scales.rearrange("g b n -> b g n").bitcast(I32))
         load_x_words(0)
         load_w1(1)
-        nc.sync.dma_start(slot_t[:], slot)
-        nc.sync.dma_start(out=drag_t[:], in_=drag)
         nc.vector.tensor_copy(picked_rows[:], x_scale_t[:, 0:T].indirect(offs_t[:]))
-        for q in range(P // QUADRANT):
+        for q in (0, 2, 1, 3):
             nc.sync.dma_start(out=picked_scales[QUADRANT * q:QUADRANT * q + SCALE_ROWS, :, :].bitcast(I32),
                               in_=picked_rows[QUADRANT * q:QUADRANT * (q + 1):SCALE_ROWS, :].bitcast(I32))
         load_x_words(1)
         nc.sync.dma_start(out=bias_t[:], in_=bias.rearrange("(p t) o -> p (t o)", t=PACK))
+        nc.sync.dma_start(slot_t[:], slot)
         nc.sync.dma_start(out=window[:], in_=mom)
-        nc.sync.dma_start(out=top_t[:], in_=top.rearrange("(p t) o -> p (t o)", t=PACK))
         nc.sync.dma_start(out=w2_raw[:], in_=w2.rearrange("(p j) n -> p j n", j=PACK))
+        nc.sync.dma_start(out=top_t[:], in_=top.rearrange("(p t) o -> p (t o)", t=PACK))
+        nc.sync.dma_start(out=drag_t[:], in_=drag)
 
         neg_top = tile([P, PACK], F32, "neg_top")
         nc.scalar.activation(neg_top[:], top_t[:], ACT.Copy, scale=-1.0)
         drag_kick = tile([P, 1], F32, "kick")
-        nc.vector.tensor_scalar(drag_kick[:], drag_t[:], KICK, 0.0, ALU.mult, ALU.add)
+        nc.scalar.activation(drag_kick[:], drag_t[:], ACT.Copy, scale=KICK)
         drag_wide = tile([P, CHUNK], F32, "drag_wide")
         nc.vector.tensor_scalar(drag_wide[:], drag_t[:].to_broadcast([P, CHUNK]), 1.0, 0.0, ALU.mult, ALU.add)
 

@@ -119,19 +119,25 @@ def tile_picked_yham_drag_p_kernel(
         w2_scales = tile([P, N], U8, "w2_s")
 
         picked_words = [[tile([P, HALF], U32, f"gx{g}_{a}") for a in range(HALVES)] for g in range(PASSES)]
-        pre = [[ps.tile([P, HALF], F32, name=f"pre{a}_{t}", tag=f"bank{a}_{t}") for t in range(PACK)]
-               for a in range(HALVES)]
+
+        def first_product(pre, g, t, first, count):
+            a, at = divmod(first, HALF)
+            nc.tensor.matmul_mx(
+                out=pre[:],
+                lhsT=w1_codes[g][:, t * P:(t + 1) * P].bitcast(FP8X4),
+                lhsT_scale=w1_scales[g][:, t * P:(t + 1) * P],
+                rhs=picked_words[g][a][:, at:at + count].bitcast(FP8X4),
+                rhs_scale=picked_scales[:, g, first:first + count],
+                start=(g == 0), stop=(g == PASSES - 1))
+
+        pre = [[ps.tile([P, CHUNK], F32, name=f"pre{c}_{t}", tag=f"bank{c}_{t}") for t in range(PACK)]
+               for c in range(2)]
         for g in range(PASSES):
             for a in range(HALVES):
                 nc.vector.tensor_copy(picked_words[g][a][:], x_word_t[g][:].indirect(entries(offs_t, a * HALF, HALF)))
+            for c in range(2):
                 for t in range(PACK):
-                    nc.tensor.matmul_mx(
-                        out=pre[a][t][:],
-                        lhsT=w1_codes[g][:, t * P:(t + 1) * P].bitcast(FP8X4),
-                        lhsT_scale=w1_scales[g][:, t * P:(t + 1) * P],
-                        rhs=picked_words[g][a][:].bitcast(FP8X4),
-                        rhs_scale=picked_scales[:, g, a * HALF:(a + 1) * HALF],
-                        start=(g == 0), stop=(g == PASSES - 1))
+                    first_product(pre[c][t], g, t, c * CHUNK, CHUNK)
 
         mom_picked = tile([P, S], F32, "mom_g")
         nc.vector.tensor_copy(mom_picked[:], window[:].indirect(slot_t[:]))
@@ -147,12 +153,17 @@ def tile_picked_yham_drag_p_kernel(
             if c == 2:
                 wide.append(tile([P, PACK, HALF], F32, "h2"))
                 for t in range(PACK):
-                    nc.scalar.activation(wide[0][:, t, :], pre[a][t][:], ACT.Tanh, bias=bias_t[:, t:t + 1])
+                    nc.scalar.activation(wide[0][:, t, :], pre[2][t][:], ACT.Tanh, bias=bias_t[:, t:t + 1])
             if c >= 2:
                 return wide[0][:, :, first:first + CHUNK]
             h = tile([P, PACK, CHUNK], F32, f"h{c}")
             for t in range(PACK):
-                nc.scalar.activation(h[:, t, :], pre[a][t][:, first:first + CHUNK], ACT.Tanh, bias=bias_t[:, t:t + 1])
+                nc.scalar.activation(h[:, t, :], pre[c][t][:], ACT.Tanh, bias=bias_t[:, t:t + 1])
+            if c == 0:
+                pre.append([ps.tile([P, HALF], F32, name=f"pre2_{t}", tag=f"bank0_{t}") for t in range(PACK)])
+                for t in range(PACK):
+                    for g in range(PASSES):
+                        first_product(pre[2][t], g, t, HALF, HALF)
             return h
 
         def quantize_z(z_bf, z_codes, z_scales):
@@ -175,10 +186,14 @@ def tile_picked_yham_drag_p_kernel(
                     else tile([P, CHUNK, PACK], BF16, f"z_b{c}", "hh0"))
             z_codes = tile([P, CHUNK], U32, f"z_c{c}")
             z_scales = tile([P, CHUNK], U8, f"z_s{c}")
-            nc.scalar.activation(hh[:].rearrange("p (c i) t -> p c t i", i=4),
-                                 h[:].rearrange("p t (c i) -> p c t i", i=4), ACT.Square)
-            nc.vector.scalar_tensor_tensor(z_bf[:], hh[:], 1.0, top_t[:].unsqueeze(1).to_broadcast([P, CHUNK, PACK]),
-                                           ALU.subtract, ALU.mult)
+            part = CHUNK if c == 0 else CHUNK // 2
+            for first in range(0, CHUNK, part):
+                cols = slice(first, first + part)
+                nc.scalar.activation(hh[:, cols, :].rearrange("p (c i) t -> p c t i", i=4),
+                                     h[:, :, cols].rearrange("p t (c i) -> p c t i", i=4), ACT.Square)
+                nc.vector.scalar_tensor_tensor(z_bf[:, cols, :], hh[:, cols, :], 1.0,
+                                               top_t[:].unsqueeze(1).to_broadcast([P, part, PACK]),
+                                               ALU.subtract, ALU.mult)
             return quantize_z(z_bf, z_codes, z_scales)
 
         def z_on_scalar(c):
@@ -198,7 +213,7 @@ def tile_picked_yham_drag_p_kernel(
             return quantize_z(z_bf, z_codes, z_scales)
 
         def second_product(c, z_codes, z_scales):
-            y = ps.tile([P, CHUNK], F32, name=f"y{c}", tag=f"bank0_{c}")
+            y = ps.tile([P, CHUNK], F32, name=f"y{c}", tag=f"bank1_{c}")
             nc.tensor.matmul_mx(out=y[:], lhsT=w2_codes[:].bitcast(FP8X4), lhsT_scale=w2_scales[:],
                                 rhs=z_codes[:].bitcast(FP8X4), rhs_scale=z_scales[:], start=True, stop=True)
             return y

@@ -118,31 +118,31 @@ def tile_picked_yham_drag_p_kernel(
         w2_codes = tile([P, N], U32, "w2_c")
         w2_scales = tile([P, N], U8, "w2_s")
 
-        picked_words = [[tile([P, HALF], U32, f"gx{g}_{a}") for a in range(HALVES)] for g in range(PASSES)]
+        picked_words = [tile([P, S], U32, f"gx{g}") for g in range(PASSES)]
 
         def first_product(pre, g, t, first, count):
-            a, at = divmod(first, HALF)
             nc.tensor.matmul_mx(
                 out=pre[:],
                 lhsT=w1_codes[g][:, t * P:(t + 1) * P].bitcast(FP8X4),
                 lhsT_scale=w1_scales[g][:, t * P:(t + 1) * P],
-                rhs=picked_words[g][a][:, at:at + count].bitcast(FP8X4),
+                rhs=picked_words[g][:, first:first + count].bitcast(FP8X4),
                 rhs_scale=picked_scales[:, g, first:first + count],
                 start=(g == 0), stop=(g == PASSES - 1))
 
         pre = [[ps.tile([P, CHUNK], F32, name=f"pre{c}_{t}", tag=f"bank{c}_{t}") for t in range(PACK)]
                for c in range(2)]
         for g in range(PASSES):
-            for a in range(HALVES):
-                nc.vector.tensor_copy(picked_words[g][a][:], x_word_t[g][:].indirect(entries(offs_t, a * HALF, HALF)))
+            for first, count in ((0, CHUNK), (CHUNK, S - CHUNK)):
+                nc.vector.tensor_copy(picked_words[g][:, first:first + count],
+                                      x_word_t[g][:].indirect(entries(offs_t, first, count)))
             for c in range(2):
                 for t in range(PACK):
                     first_product(pre[c][t], g, t, c * CHUNK, CHUNK)
 
         mom_picked = tile([P, S], F32, "mom_g")
         nc.vector.tensor_copy(mom_picked[:], window[:].indirect(slot_t[:]))
-        nc.vector.tensor_copy(w2_bf[:].rearrange("p (c i j) -> p c j i", i=4, j=PACK),
-                              w2_raw[:].rearrange("p j (c i) -> p c j i", i=4))
+        nc.gpsimd.tensor_scalar(w2_bf[:].rearrange("p (n j) -> p n j", j=PACK), w2_raw[:].rearrange("p j n -> p n j"),
+                                1.0, 0.0, ALU.mult, ALU.add)
         nc.vector.quantize_mx(out=w2_codes[:].bitcast(FP8X4), scales=w2_scales[:], in_=w2_bf[:])
 
         wide = []

@@ -132,7 +132,7 @@ def tile_picked_yham_drag_p_kernel(
         pre = [[ps.tile([P, CHUNK], F32, name=f"pre{c}_{t}", tag=f"bank{c}_{t}") for t in range(PACK)]
                for c in range(2)]
         for g in range(PASSES):
-            for first, count in ((0, CHUNK), (CHUNK, S - CHUNK)):
+            for first, count in ((0, CHUNK), (CHUNK, CHUNK), (HALF, HALF)):
                 nc.vector.tensor_copy(picked_words[g][:, first:first + count],
                                       x_word_t[g][:].indirect(entries(offs_t, first, count)))
             for c in range(2):

@@ -143,7 +143,6 @@ def tile_picked_yham_drag_p_kernel(
         nc.vector.tensor_copy(mom_picked[:], window[:].indirect(slot_t[:]))
         nc.gpsimd.tensor_scalar(w2_bf[:].rearrange("p (n j) -> p n j", j=PACK), w2_raw[:].rearrange("p j n -> p n j"),
                                 1.0, 0.0, ALU.mult, ALU.add)
-        nc.vector.quantize_mx(out=w2_codes[:].bitcast(FP8X4), scales=w2_scales[:], in_=w2_bf[:])
 
         wide = []
         kept_list = []
@@ -182,7 +181,7 @@ def tile_picked_yham_drag_p_kernel(
             if c == 2:
                 square_last(0)
             hh = tile([P, CHUNK, PACK], F32, f"hh{c}")
-            z_bf = (placed([P, CHUNK, PACK], BF16, "z_b0", W2_AT, "w2_raw") if c == 0
+            z_bf = (tile([P, CHUNK, PACK], BF16, "z_b0") if c == 0
                     else tile([P, CHUNK, PACK], BF16, f"z_b{c}", "hh0"))
             z_codes = tile([P, CHUNK], U32, f"z_c{c}")
             z_scales = tile([P, CHUNK], U8, f"z_s{c}")
@@ -194,6 +193,8 @@ def tile_picked_yham_drag_p_kernel(
                 nc.vector.scalar_tensor_tensor(z_bf[:, cols, :], hh[:, cols, :], 1.0,
                                                top_t[:].unsqueeze(1).to_broadcast([P, part, PACK]),
                                                ALU.subtract, ALU.mult)
+            if c == 0:
+                nc.vector.quantize_mx(out=w2_codes[:].bitcast(FP8X4), scales=w2_scales[:], in_=w2_bf[:])
             return quantize_z(z_bf, z_codes, z_scales)
 
         def z_on_scalar(c):

@@ -25,12 +25,9 @@ LIST_ROWS = 16
 PAIRS = 2
 PAIR = PACK // PAIRS
 HALF = 256
-HALVES = S // HALF
 CHUNK = 128
 CHUNKS = S // CHUNK
-LAST = CHUNKS - 1
-SCALAR_EMPTIES_FROM = 2
-W2_AT = 15168
+RUN = 4
 KICK = 0.4
 
 
@@ -43,8 +40,8 @@ def tile_picked_yham_drag_p_kernel(
         ps = ctx.enter_context(tc.psum_pool(name="ps", bufs=1))
         laid = ctx.enter_context(tc.tile_pool(name="laid", bufs=1))
 
-        def placed(shape, dtype, name, offset, tag=None):
-            return laid.tile(shape, dtype, name=name, tag=tag or name, align_bytes=64, offset=offset)
+        def placed(shape, dtype, name, offset):
+            return laid.tile(shape, dtype, name=name, align_bytes=64, offset=offset)
 
         def tile(shape, dtype, name, tag=None):
             return sb.tile(shape, dtype, name=name, tag=tag or name, align_bytes=64)
@@ -57,13 +54,13 @@ def tile_picked_yham_drag_p_kernel(
         w1_raw = [tile([P, PACK, H], F32, f"w1_raw{g}") for g in range(PASSES)]
         x_word_t = [tile([P, T], U32, "xw0"), placed([P, T], U32, "xw1", 0)]
         x_scale_t = placed([P, T + 512], U8, "xs", 8128)
-        bias_t = placed([P, PACK], F32, "bias_t", 8192)
-        top_t = placed([P, PACK], F32, "top_t", 8256)
-        drag_t = placed([P, 1], F32, "drag_t", 10432)
-        window = placed([P, U], F32, "window", 10624)
-        picked_rows = placed([P, S], U8, "picked_rows", 14720)
-        w2_raw = placed([P, PACK, N], F32, "w2_raw", W2_AT)
+        w2_raw = placed([P, PACK, N], F32, "w2_raw", 10624)
+        picked_rows = placed([P, S], U8, "picked_rows", 12672)
+        window = placed([P, U], F32, "window", 13120)
         picked_scales = tile([P, PASSES, S], U8, "gs")
+        bias_t = tile([P, PACK], F32, "bias_t")
+        top_t = tile([P, PACK], F32, "top_t")
+        drag_t = tile([P, 1], F32, "drag_t")
 
         def load_w1(g):
             rows = w1[g * K_PASS:(g + 1) * K_PASS, :]
@@ -86,19 +83,17 @@ def tile_picked_yham_drag_p_kernel(
             nc.sync.dma_start(out=picked_scales[QUADRANT * q:QUADRANT * q + SCALE_ROWS, :, :].bitcast(I32),
                               in_=picked_rows[QUADRANT * q:QUADRANT * (q + 1):SCALE_ROWS, :].bitcast(I32))
         load_x_words(1)
-        nc.sync.dma_start(out=bias_t[:], in_=bias.rearrange("(p t) o -> p (t o)", t=PACK))
+        nc.sync.dma_start(out=w2_raw[:], in_=w2.rearrange("(p j) n -> p j n", j=PACK))
         nc.sync.dma_start(slot_t[:], slot)
         nc.sync.dma_start(out=window[:], in_=mom)
-        nc.sync.dma_start(out=w2_raw[:], in_=w2.rearrange("(p j) n -> p j n", j=PACK))
-        nc.sync.dma_start(out=top_t[:], in_=top.rearrange("(p t) o -> p (t o)", t=PACK))
-        nc.sync.dma_start(out=drag_t[:], in_=drag)
 
+        nc.gpsimd.dma_start(out=bias_t[:], in_=bias.rearrange("(p t) o -> p (t o)", t=PACK))
+        nc.gpsimd.dma_start(out=top_t[:], in_=top.rearrange("(p t) o -> p (t o)", t=PACK))
+        nc.gpsimd.dma_start(out=drag_t[:], in_=drag)
         neg_top = tile([P, PACK], F32, "neg_top")
-        nc.scalar.activation(neg_top[:], top_t[:], ACT.Copy, scale=-1.0)
-        drag_kick = tile([P, 1], F32, "kick")
-        nc.scalar.activation(drag_kick[:], drag_t[:], ACT.Copy, scale=KICK)
-        drag_wide = tile([P, CHUNK], F32, "drag_wide")
-        nc.vector.tensor_scalar(drag_wide[:], drag_t[:].to_broadcast([P, CHUNK]), 1.0, 0.0, ALU.mult, ALU.add)
+        drag_kick = tile([P, 1], F32, "drag_kick")
+        nc.gpsimd.tensor_scalar(neg_top[:], top_t[:], -1.0, 0.0, ALU.mult, ALU.add)
+        nc.gpsimd.tensor_scalar(drag_kick[:], drag_t[:], -KICK, 0.0, ALU.mult, ALU.add)
 
         w1_codes = [tile([P, H], U32, f"w1_c{g}") for g in range(PASSES)]
         w1_scales = [tile([P, H], U8, f"w1_s{g}") for g in range(PASSES)]
@@ -114,132 +109,117 @@ def tile_picked_yham_drag_p_kernel(
                 nc.vector.quantize_mx(out=w1_codes[g][:, cols].bitcast(FP8X4), scales=w1_scales[g][:, cols],
                                       in_=w1_bf[u][:])
 
-        w2_bf = tile([P, N * PACK], BF16, "w2_b")
-        w2_codes = tile([P, N], U32, "w2_c")
-        w2_scales = tile([P, N], U8, "w2_s")
-
         picked_words = [tile([P, S], U32, f"gx{g}") for g in range(PASSES)]
 
-        def first_product(pre, g, t, first, count):
+        def first_product(pre, g, t, first, count, start, stop):
             nc.tensor.matmul_mx(
-                out=pre[:],
+                out=pre,
                 lhsT=w1_codes[g][:, t * P:(t + 1) * P].bitcast(FP8X4),
                 lhsT_scale=w1_scales[g][:, t * P:(t + 1) * P],
                 rhs=picked_words[g][:, first:first + count].bitcast(FP8X4),
                 rhs_scale=picked_scales[:, g, first:first + count],
-                start=(g == 0), stop=(g == PASSES - 1))
+                start=start, stop=stop)
 
-        pre = [[ps.tile([P, CHUNK], F32, name=f"pre{c}_{t}", tag=f"bank{c}_{t}") for t in range(PACK)]
-               for c in range(2)]
+        pieces = ((0, CHUNK, 1), (CHUNK, CHUNK, PACK), (HALF, HALF, PAIR))
+        banks = [[ps.tile([P, shared, count], F32, name=f"pre{a}_{b}", tag=f"bank{a}_{b}")
+                  for b in range(PACK // shared)] for a, (first, count, shared) in enumerate(pieces)]
+        pre = [[banks[a][t // shared][:, t % shared, :] for t in range(PACK)]
+               for a, (first, count, shared) in enumerate(pieces)]
         for g in range(PASSES):
-            for first, count in ((0, CHUNK), (CHUNK, CHUNK), (HALF, HALF)):
+            for a, (first, count, shared) in enumerate(pieces):
                 nc.vector.tensor_copy(picked_words[g][:, first:first + count],
                                       x_word_t[g][:].indirect(entries(offs_t, first, count)))
-            for c in range(2):
                 for t in range(PACK):
-                    first_product(pre[c][t], g, t, c * CHUNK, CHUNK)
+                    first_product(pre[a][t], g, t, first, count, g == 0 and t % shared == 0,
+                                  g == PASSES - 1 and t % shared == shared - 1)
 
-        mom_picked = tile([P, S], F32, "mom_g")
-        nc.vector.tensor_copy(mom_picked[:], window[:].indirect(slot_t[:]))
+        w2_bf = tile([P, N * PACK], BF16, "w2_b")
+        w2_codes = tile([P, N], U32, "w2_c")
+        w2_scales = tile([P, N], U8, "w2_s")
         nc.gpsimd.tensor_scalar(w2_bf[:].rearrange("p (n j) -> p n j", j=PACK), w2_raw[:].rearrange("p j n -> p n j"),
                                 1.0, 0.0, ALU.mult, ALU.add)
 
-        wide = []
-        kept_list = []
-
-        def tanh_chunk(c):
-            a, first = divmod(c * CHUNK, HALF)
-            if c == 2:
-                wide.append(tile([P, PACK, HALF], F32, "h2"))
-                for t in range(PACK):
-                    nc.scalar.activation(wide[0][:, t, :], pre[2][t][:], ACT.Tanh, bias=bias_t[:, t:t + 1])
-            if c >= 2:
-                return wide[0][:, :, first:first + CHUNK]
-            h = tile([P, PACK, CHUNK], F32, f"h{c}")
+        def sigmoid(sums, width, name):
+            s = tile([P, width // RUN, PACK, RUN], F32, name)
             for t in range(PACK):
-                nc.scalar.activation(h[:, t, :], pre[c][t][:], ACT.Tanh, bias=bias_t[:, t:t + 1])
-            if c == 0:
-                pre.append([ps.tile([P, HALF], F32, name=f"pre2_{t}", tag=f"bank0_{t}") for t in range(PACK)])
-                for t in range(PACK):
-                    for g in range(PASSES):
-                        first_product(pre[2][t], g, t, HALF, HALF)
-            return h
+                nc.scalar.activation(s[:, :, t, :], sums[t].rearrange("p (c i) -> p c i", i=RUN), ACT.Tanh,
+                                     bias=bias_t[:, t:t + 1])
+            return s
 
-        def quantize_z(z_bf, z_codes, z_scales):
-            nc.vector.quantize_mx(out=z_codes[:].bitcast(FP8X4), scales=z_scales[:],
-                                  in_=z_bf[:].rearrange("p j t -> p (j t)"))
-            return z_codes, z_scales
+        def rest(s, width, name):
+            m = tile([P, width // RUN, PACK, RUN], F32, name)
+            for t in range(PACK):
+                nc.vector.tensor_scalar(m[:, :, t, :], s[:, :, t, :], neg_top[:, t:t + 1], top_t[:, t:t + 1],
+                                        ALU.mult, ALU.add)
+            return m
 
-        hh_last = tile([P, PACK, CHUNK], F32, "hh_last")
+        def weave(c, s, m):
+            z_bf = tile([P, RUN, CHUNK // RUN, PACK], BF16, f"z_b{c}", {2: "mom_g0", 3: "kept0"}.get(c))
+            nc.vector.scalar_tensor_tensor(z_bf[:].rearrange("p i c t -> p (c t) i"),
+                                           s.rearrange("p c t i -> p (c t) i"), 1.0,
+                                           m.rearrange("p c t i -> p (c t) i"), ALU.add, ALU.mult)
+            return z_bf
 
-        def square_last(u):
-            groups = slice(u * PAIR, (u + 1) * PAIR)
-            nc.scalar.activation(hh_last[:, groups, :], wide[0][:, groups, CHUNK:HALF], ACT.Square)
-
-        def z_shared(c):
-            h = tanh_chunk(c)
-            if c == 2:
-                square_last(0)
-            hh = tile([P, CHUNK, PACK], F32, f"hh{c}")
-            z_bf = (tile([P, CHUNK, PACK], BF16, "z_b0") if c == 0
-                    else tile([P, CHUNK, PACK], BF16, f"z_b{c}", "hh0"))
+        def product(c, z_bf):
             z_codes = tile([P, CHUNK], U32, f"z_c{c}")
             z_scales = tile([P, CHUNK], U8, f"z_s{c}")
-            part = CHUNK if c == 0 else CHUNK // 2
-            for first in range(0, CHUNK, part):
-                cols = slice(first, first + part)
-                nc.scalar.activation(hh[:, cols, :].rearrange("p (c i) t -> p c t i", i=4),
-                                     h[:, :, cols].rearrange("p t (c i) -> p c t i", i=4), ACT.Square)
-                nc.vector.scalar_tensor_tensor(z_bf[:, cols, :], hh[:, cols, :], 1.0,
-                                               top_t[:].unsqueeze(1).to_broadcast([P, part, PACK]),
-                                               ALU.subtract, ALU.mult)
-            if c == 0:
-                nc.vector.quantize_mx(out=w2_codes[:].bitcast(FP8X4), scales=w2_scales[:], in_=w2_bf[:])
-            return quantize_z(z_bf, z_codes, z_scales)
-
-        def z_on_scalar(c):
-            hh = hh_last
-            square_last(1)
-            z_groups = tile([P, PACK, CHUNK], BF16, "z_rows")
-            for t in range(PACK):
-                nc.scalar.activation(z_groups[:, t, :], hh[:, t, :], ACT.Identity,
-                                     bias=neg_top[:, t:t + 1], scale=top_t[:, t:t + 1])
-            kept_all = tile([P, S - SCALAR_EMPTIES_FROM * CHUNK], F32, "kept", "h2")
-            nc.scalar.activation(kept_all[:], mom_picked[:, SCALAR_EMPTIES_FROM * CHUNK:], ACT.Copy, scale=drag_t[:])
-            kept_list.append(kept_all)
-            z_bf = tile([P, CHUNK, PACK], BF16, f"z_b{c}")
-            nc.scalar.copy(z_bf[:].rearrange("p (c i) t -> p c t i", i=4), z_groups[:].rearrange("p t (c i) -> p c t i", i=4))
-            z_codes = tile([P, CHUNK], U32, f"z_c{c}", "hh0")
-            z_scales = tile([P, CHUNK], U8, f"z_s{c}")
-            return quantize_z(z_bf, z_codes, z_scales)
-
-        def second_product(c, z_codes, z_scales):
-            y = ps.tile([P, CHUNK], F32, name=f"y{c}", tag=f"bank1_{c}")
+            nc.vector.quantize_mx(out=z_codes[:].bitcast(FP8X4), scales=z_scales[:],
+                                  in_=z_bf[:].rearrange("p i c t -> p (i c t)"))
+            y = ps.tile([P, CHUNK], F32, name=f"y{c}", tag=f"bank0_{c}")
             nc.tensor.matmul_mx(out=y[:], lhsT=w2_codes[:].bitcast(FP8X4), lhsT_scale=w2_scales[:],
                                 rhs=z_codes[:].bitcast(FP8X4), rhs_scale=z_scales[:], start=True, stop=True)
             return y
 
-        def put_from_vector(c, z):
-            y = second_product(c, *z)
-            p = tile([P, CHUNK], F32, f"p{c}", "h1" if c == 0 else "hh1")
-            nc.vector.scalar_tensor_tensor(p[:], y[:], KICK, mom_picked[:, c * CHUNK:(c + 1) * CHUNK],
+        def look_up(a):
+            picked = tile([P, HALF], F32, f"mom_g{a}")
+            nc.scalar.activation(picked[:], window[:].indirect(entries(slot_t, a * HALF, HALF)), ACT.Copy)
+            return picked
+
+        def dragged(kept, picked):
+            nc.vector.tensor_scalar(kept, picked[:], drag_t[:], 0.0, ALU.mult, ALU.add)
+            return kept
+
+        new = tile([P, S], F32, "new")
+
+        def kick(c, y, kept):
+            first = c * CHUNK % HALF
+            nc.vector.scalar_tensor_tensor(new[:, c * CHUNK:(c + 1) * CHUNK].rearrange("p (c i) -> p c i", i=RUN),
+                                           y[:].rearrange("p (i c) -> p c i", i=RUN), drag_kick[:],
+                                           kept[:, first:first + CHUNK].rearrange("p (c i) -> p c i", i=RUN),
                                            ALU.mult, ALU.add)
-            nc.vector.tensor_tensor(window[:].indirect(entries(slot_t, c * CHUNK, CHUNK)), p[:], drag_wide[:],
-                                    ALU.mult)
 
-        def put_from_scalar(c, z, kept):
-            y = second_product(c, *z)
-            kicked = tile([P, CHUNK], F32, f"kicked{c}", "hh_last" if c < LAST else None)
-            nc.scalar.activation(kicked[:], y[:], ACT.Copy, scale=drag_kick[:])
-            nc.vector.tensor_tensor(window[:].indirect(entries(slot_t, c * CHUNK, CHUNK)), kept, kicked[:], ALU.add)
+        def put(first, count):
+            nc.scalar.activation(window[:].indirect(entries(slot_t, first, count)), new[:, first:first + count],
+                                 ACT.Copy)
 
-        z = [z_shared(0)]
-        for c in range(1, LAST):
-            z.append(z_shared(c))
-            put_from_vector(c - 1, z[c - 1])
-        z.append(z_on_scalar(LAST))
-        kept_all = kept_list[0]
-        for i, c in enumerate(range(SCALAR_EMPTIES_FROM, CHUNKS)):
-            put_from_scalar(c, z[c], kept_all[:, i * CHUNK:(i + 1) * CHUNK])
+        s0 = sigmoid(pre[0], CHUNK, "s0")
+        s1 = sigmoid(pre[1], CHUNK, "s1")
+        s2 = sigmoid(pre[2], HALF, "s2")
+        g0 = look_up(0)
+        g1 = look_up(1)
+
+        m0 = rest(s0, CHUNK, "m0")
+        nc.vector.quantize_mx(out=w2_codes[:].bitcast(FP8X4), scales=w2_scales[:], in_=w2_bf[:])
+        z0 = weave(0, s0[:], m0[:])
+        m1 = rest(s1, CHUNK, "m1")
+        y0 = product(0, z0)
+        z1 = weave(1, s1[:], m1[:])
+        m2 = rest(s2, HALF, "m2")
+        y1 = product(1, z1)
+        kept = [tile([P, HALF], F32, f"kept{a}") for a in range(2)]
+        kept0 = dragged(kept[0][:], g0)
+        kept1 = dragged(kept[1][:], g1)
+        kick(0, y0, kept0)
+        put(0, CHUNK)
+        z2 = weave(2, s2[:, 0:CHUNK // RUN], m2[:, 0:CHUNK // RUN])
+        kick(1, y1, kept0)
+        put(CHUNK, CHUNK)
+        y2 = product(2, z2)
+        z3 = weave(3, s2[:, CHUNK // RUN:], m2[:, CHUNK // RUN:])
+        kick(2, y2, kept1)
+        put(2 * CHUNK, CHUNK)
+        y3 = product(3, z3)
+        kick(3, y3, kept1)
+        put(3 * CHUNK, CHUNK)
 
         nc.sync.dma_start(out=out, in_=window[:])

@@ -53,11 +53,11 @@ def tile_picked_yham_drag_p_kernel(
         slot_t = sb.tile([P, S // LIST_ROWS], U16, name="slot_t")
         w1_raw = [tile([P, PACK, H], F32, f"w1_raw{g}") for g in range(PASSES)]
         x_word_t = [tile([P, T], U32, "xw0"), placed([P, T], U32, "xw1", 0)]
-        x_scale_t = placed([P, T + 512], U8, "xs", 8128)
+        x_scale_t = placed([P, T + 2560], U8, "xs", 8128)
         w2_raw = placed([P, PACK, N], F32, "w2_raw", 10624)
-        picked_rows = placed([P, S], U8, "picked_rows", 12672)
-        window = placed([P, U], F32, "window", 13120)
-        picked_scales = tile([P, PASSES, S], U8, "gs")
+        picked_rows = tile([P, S], U8, "picked_rows")
+        window = placed([P, U], F32, "window", 12672)
+        picked_scales = [tile([P, S], U8, f"gs{g}") for g in range(PASSES)]
         bias_t = tile([P, PACK], F32, "bias_t")
         top_t = tile([P, PACK], F32, "top_t")
         drag_t = tile([P, 1], F32, "drag_t")
@@ -71,7 +71,8 @@ def tile_picked_yham_drag_p_kernel(
                               in_=x_words[g].rearrange("p n j -> p (n j)").bitcast(I32))
 
         nc.vector.memset(x_scale_t[:, 0:T].bitcast(I32), 0)
-        nc.vector.memset(picked_scales[:].rearrange("p g s -> p (g s)").bitcast(I32), 0)
+        for g in range(PASSES):
+            nc.vector.memset(picked_scales[g][:].bitcast(I32), 0)
         load_w1(0)
         nc.sync.dma_start(offs_t[:], offs)
         nc.sync.dma_start(out=x_scale_t[0:P:SCALE_ROWS, 0:T].bitcast(I32),
@@ -79,10 +80,16 @@ def tile_picked_yham_drag_p_kernel(
         load_x_words(0)
         load_w1(1)
         nc.vector.tensor_copy(picked_rows[:], x_scale_t[:, 0:T].indirect(offs_t[:]))
-        for q in (0, 2, 1, 3):
-            nc.sync.dma_start(out=picked_scales[QUADRANT * q:QUADRANT * q + SCALE_ROWS, :, :].bitcast(I32),
-                              in_=picked_rows[QUADRANT * q:QUADRANT * (q + 1):SCALE_ROWS, :].bitcast(I32))
+
+        def move_scales(g):
+            for q in (0, 2, 1, 3):
+                first = QUADRANT * q + SCALE_ROWS * g
+                nc.sync.dma_start(out=picked_scales[g][QUADRANT * q:QUADRANT * q + SCALE_ROWS, :].bitcast(I32),
+                                  in_=picked_rows[first:QUADRANT * (q + 1):PASSES * SCALE_ROWS, :].bitcast(I32))
+
+        move_scales(0)
         load_x_words(1)
+        move_scales(1)
         nc.sync.dma_start(out=w2_raw[:], in_=w2.rearrange("(p j) n -> p j n", j=PACK))
         nc.sync.dma_start(slot_t[:], slot)
         nc.sync.dma_start(out=window[:], in_=mom)
@@ -117,7 +124,7 @@ def tile_picked_yham_drag_p_kernel(
                 lhsT=w1_codes[g][:, t * P:(t + 1) * P].bitcast(FP8X4),
                 lhsT_scale=w1_scales[g][:, t * P:(t + 1) * P],
                 rhs=picked_words[g][:, first:first + count].bitcast(FP8X4),
-                rhs_scale=picked_scales[:, g, first:first + count],
+                rhs_scale=picked_scales[g][:, first:first + count],
                 start=start, stop=stop)
 
         pieces = ((0, CHUNK, 1), (CHUNK, CHUNK, PACK), (HALF, HALF, PAIR))

@@ -26,9 +26,8 @@ PAIRS = 2
 PAIR = PACK // PAIRS
 HALF = 256
 CHUNK = 128
-CHUNKS = S // CHUNK
-RUN = 4
 KICK = 0.4
+KIB = 1024
 
 
 def tile_picked_yham_drag_p_kernel(
@@ -51,16 +50,18 @@ def tile_picked_yham_drag_p_kernel(
 
         offs_t = sb.tile([P, S // LIST_ROWS], U16, name="offs_t")
         slot_t = sb.tile([P, S // LIST_ROWS], U16, name="slot_t")
-        w1_raw = [tile([P, PACK, H], F32, f"w1_raw{g}") for g in range(PASSES)]
-        x_word_t = [tile([P, T], U32, "xw0"), placed([P, T], U32, "xw1", 0)]
-        x_scale_t = placed([P, T + 2560], U8, "xs", 8128)
-        w2_raw = placed([P, PACK, N], F32, "w2_raw", 10624)
+        x_word_t = [placed([P, T], U32, "xw0", 12 * KIB), placed([P, T], U32, "xw1", 0)]
+        x_scale_t = placed([P, T], U8, "xs", 8 * KIB - 64)
+        w1_first = placed([P, PAIR * P * PACK], BF16, "w1_first", 10 * KIB - 128)
+        table = placed([P, U], F32, "table", 12 * KIB)
+        window = placed([P, U], F32, "window", 16 * KIB)
+        w1_raw = [placed([P, PACK, H], F32, "w1_raw0", 20 * KIB), tile([P, PACK, H], F32, "w1_raw1")]
+        w2_raw = placed([P, PACK, N], F32, "w2_raw", 20 * KIB)
         picked_rows = tile([P, S], U8, "picked_rows")
-        window = placed([P, U], F32, "window", 12672)
         picked_scales = [tile([P, S], U8, f"gs{g}") for g in range(PASSES)]
         bias_t = tile([P, PACK], F32, "bias_t")
         top_t = tile([P, PACK], F32, "top_t")
-        drag_t = tile([P, 1], F32, "drag_t")
+        drag_t = placed([P, 32], F32, "drag_t", 32 * KIB - 64)
 
         def load_w1(g):
             rows = w1[g * K_PASS:(g + 1) * K_PASS, :]
@@ -70,43 +71,48 @@ def tile_picked_yham_drag_p_kernel(
             nc.sync.dma_start(out=x_word_t[g][:].bitcast(I32),
                               in_=x_words[g].rearrange("p n j -> p (n j)").bitcast(I32))
 
-        nc.vector.memset(x_scale_t[:, 0:T].bitcast(I32), 0)
-        for g in range(PASSES):
-            nc.vector.memset(picked_scales[g][:].bitcast(I32), 0)
-        load_w1(0)
-        nc.sync.dma_start(offs_t[:], offs)
-        nc.sync.dma_start(out=x_scale_t[0:P:SCALE_ROWS, 0:T].bitcast(I32),
-                          in_=x_scales.rearrange("g b n -> b g n").bitcast(I32))
-        load_x_words(0)
-        load_w1(1)
-        nc.vector.tensor_copy(picked_rows[:], x_scale_t[:, 0:T].indirect(offs_t[:]))
-
         def move_scales(g):
             for q in (0, 2, 1, 3):
                 first = QUADRANT * q + SCALE_ROWS * g
                 nc.sync.dma_start(out=picked_scales[g][QUADRANT * q:QUADRANT * q + SCALE_ROWS, :].bitcast(I32),
                                   in_=picked_rows[first:QUADRANT * (q + 1):PASSES * SCALE_ROWS, :].bitcast(I32))
 
+        warm_in = tile([P, 1], F32, "warm_in")
+        warm_out = tile([P, 1], F32, "warm_out")
+        nc.gpsimd.memset(warm_in[:], 0.0)
+        nc.scalar.activation(warm_out[:], warm_in[:], ACT.Sigmoid)
+        nc.vector.memset(x_scale_t[:].bitcast(I32), 0)
+        for g in range(PASSES):
+            nc.vector.memset(picked_scales[g][:].bitcast(I32), 0)
+        load_w1(0)
+        nc.sync.dma_start(offs_t[:], offs)
+        nc.sync.dma_start(out=x_scale_t[0:P:SCALE_ROWS, :].bitcast(I32),
+                          in_=x_scales.rearrange("g b n -> b g n").bitcast(I32))
+        load_x_words(0)
+        load_w1(1)
+        nc.vector.tensor_copy(picked_rows[:], x_scale_t[:].indirect(offs_t[:]))
         move_scales(0)
         load_x_words(1)
         move_scales(1)
-        nc.sync.dma_start(out=w2_raw[:], in_=w2.rearrange("(p j) n -> p j n", j=PACK))
-        nc.sync.dma_start(slot_t[:], slot)
-        nc.sync.dma_start(out=window[:], in_=mom)
 
         nc.gpsimd.dma_start(out=bias_t[:], in_=bias.rearrange("(p t) o -> p (t o)", t=PACK))
         nc.gpsimd.dma_start(out=top_t[:], in_=top.rearrange("(p t) o -> p (t o)", t=PACK))
-        nc.gpsimd.dma_start(out=drag_t[:], in_=drag)
         neg_top = tile([P, PACK], F32, "neg_top")
         drag_kick = tile([P, 1], F32, "drag_kick")
-        nc.gpsimd.tensor_scalar(neg_top[:], top_t[:], -1.0, 0.0, ALU.mult, ALU.add)
-        nc.gpsimd.tensor_scalar(drag_kick[:], drag_t[:], -KICK, 0.0, ALU.mult, ALU.add)
+        pos_top = tile([P, PACK], F32, "pos_top")
+        twice_bias = tile([P, PACK], F32, "twice_bias")
+        nc.gpsimd.tensor_scalar(twice_bias[:], bias_t[:], 2.0, 0.0, ALU.mult, ALU.add)
+        nc.gpsimd.tensor_scalar(pos_top[:], top_t[:], 4.0, 0.0, ALU.mult, ALU.add)
+        nc.gpsimd.tensor_scalar(neg_top[:], top_t[:], -4.0, 0.0, ALU.mult, ALU.add)
+        third_top = placed([P, 1], F32, "third_top", 34 * KIB)
+        nc.gpsimd.tensor_scalar(third_top[:], top_t[:, 2:3], 4.0, 0.0, ALU.mult, ALU.add)
 
         w1_codes = [tile([P, H], U32, f"w1_c{g}") for g in range(PASSES)]
         w1_scales = [tile([P, H], U8, f"w1_s{g}") for g in range(PASSES)]
-        for g in range(PASSES):
+
+        def quantise_w1(g):
             src = w1_raw[g][:].rearrange("p j (m u v) -> p u m v j", u=PAIRS, v=PAIR)
-            w1_bf = [placed([P, PAIR * P * PACK], BF16, "w1_first", 8320) if g == 0 and u == 0
+            w1_bf = [w1_first if g == 0 and u == 0
                      else tile([P, PAIR * P * PACK], BF16, f"w1_b{g}_{u}") for u in range(PAIRS)]
             dst = [w1_bf[u][:].rearrange("p (v m j) -> p m v j", v=PAIR, j=PACK) for u in range(PAIRS)]
             nc.vector.tensor_copy(dst[0], src[:, 0])
@@ -117,116 +123,121 @@ def tile_picked_yham_drag_p_kernel(
                                       in_=w1_bf[u][:])
 
         picked_words = [tile([P, S], U32, f"gx{g}") for g in range(PASSES)]
-
-        def first_product(pre, g, t, first, count, start, stop):
-            nc.tensor.matmul_mx(
-                out=pre,
-                lhsT=w1_codes[g][:, t * P:(t + 1) * P].bitcast(FP8X4),
-                lhsT_scale=w1_scales[g][:, t * P:(t + 1) * P],
-                rhs=picked_words[g][:, first:first + count].bitcast(FP8X4),
-                rhs_scale=picked_scales[g][:, first:first + count],
-                start=start, stop=stop)
-
         pieces = ((0, CHUNK, 1), (CHUNK, CHUNK, PACK), (HALF, HALF, PAIR))
         banks = [[ps.tile([P, shared, count], F32, name=f"pre{a}_{b}", tag=f"bank{a}_{b}")
                   for b in range(PACK // shared)] for a, (first, count, shared) in enumerate(pieces)]
         pre = [[banks[a][t // shared][:, t % shared, :] for t in range(PACK)]
                for a, (first, count, shared) in enumerate(pieces)]
-        for g in range(PASSES):
+
+        def first_product(g):
             for a, (first, count, shared) in enumerate(pieces):
                 nc.vector.tensor_copy(picked_words[g][:, first:first + count],
                                       x_word_t[g][:].indirect(entries(offs_t, first, count)))
                 for t in range(PACK):
-                    first_product(pre[a][t], g, t, first, count, g == 0 and t % shared == 0,
-                                  g == PASSES - 1 and t % shared == shared - 1)
+                    nc.tensor.matmul_mx(
+                        out=pre[a][t],
+                        lhsT=w1_codes[g][:, t * P:(t + 1) * P].bitcast(FP8X4),
+                        lhsT_scale=w1_scales[g][:, t * P:(t + 1) * P],
+                        rhs=picked_words[g][:, first:first + count].bitcast(FP8X4),
+                        rhs_scale=picked_scales[g][:, first:first + count],
+                        start=g == 0 and t % shared == 0,
+                        stop=g == PASSES - 1 and t % shared == shared - 1)
+
+        quantise_w1(0)
+        first_product(0)
+        nc.sync.dma_start(out=w2_raw[:], in_=w2.rearrange("(p j) n -> p j n", j=PACK))
+        nc.sync.dma_start(slot_t[:], slot)
+        nc.sync.dma_start(out=table[:], in_=mom)
+        nc.sync.dma_start(out=drag_t[:, 0:1], in_=drag)
+        nc.sync.dma_start(out=window[:], in_=mom)
+        quantise_w1(1)
+        first_product(1)
 
         w2_bf = tile([P, N * PACK], BF16, "w2_b")
         w2_codes = tile([P, N], U32, "w2_c")
         w2_scales = tile([P, N], U8, "w2_s")
         nc.gpsimd.tensor_scalar(w2_bf[:].rearrange("p (n j) -> p n j", j=PACK), w2_raw[:].rearrange("p j n -> p n j"),
                                 1.0, 0.0, ALU.mult, ALU.add)
+        nc.gpsimd.tensor_scalar(drag_kick[:], drag_t[:, 0:1], -KICK, 0.0, ALU.mult, ALU.add)
 
-        def sigmoid(sums, width, name):
-            s = tile([P, width // RUN, PACK, RUN], F32, name)
+        def scratch(shape, dtype, name, where):
+            return placed(shape, dtype, name, where) if isinstance(where, int) else tile(shape, dtype, name, where)
+
+        def hidden(sums, width, name, where=None):
+            s = scratch([P, PACK, width], F32, name, where)
             for t in range(PACK):
-                nc.scalar.activation(s[:, :, t, :], sums[t].rearrange("p (c i) -> p c i", i=RUN), ACT.Tanh,
-                                     bias=bias_t[:, t:t + 1])
+                nc.scalar.activation(s[:, t, :], sums[t], ACT.Sigmoid, bias=twice_bias[:, t:t + 1], scale=2.0)
             return s
 
-        def rest(s, width, name):
-            m = tile([P, width // RUN, PACK, RUN], F32, name)
+        def factor(s, width, name, where=None):
+            m = scratch([P, PACK, width], F32, name, where)
             for t in range(PACK):
-                nc.vector.tensor_scalar(m[:, :, t, :], s[:, :, t, :], neg_top[:, t:t + 1], top_t[:, t:t + 1],
-                                        ALU.mult, ALU.add)
+                plus = third_top[:] if width == HALF and t == 2 else pos_top[:, t:t + 1]
+                nc.vector.tensor_scalar(m[:, t, :], s[:, t, :], neg_top[:, t:t + 1], plus, ALU.mult, ALU.add)
             return m
 
-        def weave(c, s, m):
-            z_bf = tile([P, RUN, CHUNK // RUN, PACK], BF16, f"z_b{c}", {2: "mom_g0", 3: "kept0"}.get(c))
-            nc.vector.scalar_tensor_tensor(z_bf[:].rearrange("p i c t -> p (c t) i"),
-                                           s.rearrange("p c t i -> p (c t) i"), 1.0,
-                                           m.rearrange("p c t i -> p (c t) i"), ALU.add, ALU.mult)
+        def weave(c, s, m, where=None):
+            z_bf = scratch([P, CHUNK, PACK], BF16, f"z_b{c}", where)
+            nc.vector.tensor_tensor(z_bf[:].rearrange("p (c i) t -> p c t i", i=PAIR),
+                                    s.rearrange("p t (c i) -> p c t i", i=PAIR),
+                                    m.rearrange("p t (c i) -> p c t i", i=PAIR), ALU.mult)
             return z_bf
 
-        def product(c, z_bf):
-            z_codes = tile([P, CHUNK], U32, f"z_c{c}")
+        def second_product(c, z_bf, tag=None):
+            z_codes = tile([P, CHUNK], U32, f"z_c{c}", tag)
             z_scales = tile([P, CHUNK], U8, f"z_s{c}")
             nc.vector.quantize_mx(out=z_codes[:].bitcast(FP8X4), scales=z_scales[:],
-                                  in_=z_bf[:].rearrange("p i c t -> p (i c t)"))
+                                  in_=z_bf[:].rearrange("p c t -> p (c t)"))
             y = ps.tile([P, CHUNK], F32, name=f"y{c}", tag=f"bank0_{c}")
             nc.tensor.matmul_mx(out=y[:], lhsT=w2_codes[:].bitcast(FP8X4), lhsT_scale=w2_scales[:],
                                 rhs=z_codes[:].bitcast(FP8X4), rhs_scale=z_scales[:], start=True, stop=True)
             return y
 
-        def look_up(a):
-            picked = tile([P, HALF], F32, f"mom_g{a}")
-            nc.scalar.activation(picked[:], window[:].indirect(entries(slot_t, a * HALF, HALF)), ACT.Copy)
+        def look_up(a, tag=None):
+            picked = tile([P, HALF], F32, f"mom_g{a}", tag)
+            nc.scalar.activation(picked[:], table[:].indirect(entries(slot_t, a * HALF, HALF)), ACT.Copy)
             return picked
 
-        def dragged(kept, picked):
-            nc.vector.tensor_scalar(kept, picked[:], drag_t[:], 0.0, ALU.mult, ALU.add)
+        def dragged(a, picked, tag=None):
+            kept = tile([P, HALF], F32, f"kept{a}", tag)
+            nc.vector.tensor_scalar(kept[:], picked[:], drag_kick[:], -1.0 / KICK, ALU.mult, ALU.mult)
             return kept
 
-        new = tile([P, S], F32, "new")
-
-        def kick(c, y, kept):
+        def kick(c, y, kept, where=None):
+            new = scratch([P, CHUNK], F32, f"new{c}", where)
             first = c * CHUNK % HALF
-            nc.vector.scalar_tensor_tensor(new[:, c * CHUNK:(c + 1) * CHUNK].rearrange("p (c i) -> p c i", i=RUN),
-                                           y[:].rearrange("p (i c) -> p c i", i=RUN), drag_kick[:],
-                                           kept[:, first:first + CHUNK].rearrange("p (c i) -> p c i", i=RUN),
-                                           ALU.mult, ALU.add)
+            nc.vector.scalar_tensor_tensor(new[:], y[:], drag_kick[:], kept[:, first:first + CHUNK], ALU.mult, ALU.add)
+            return new
 
-        def put(first, count):
-            nc.scalar.activation(window[:].indirect(entries(slot_t, first, count)), new[:, first:first + count],
-                                 ACT.Copy)
+        def put(c, new):
+            nc.scalar.activation(window[:].indirect(entries(slot_t, c * CHUNK, CHUNK)), new[:], ACT.Copy)
 
-        s0 = sigmoid(pre[0], CHUNK, "s0")
-        s1 = sigmoid(pre[1], CHUNK, "s1")
-        s2 = sigmoid(pre[2], HALF, "s2")
+        h0 = hidden(pre[0], CHUNK, "h0")
+        h1 = hidden(pre[1], CHUNK, "h1")
         g0 = look_up(0)
-        g1 = look_up(1)
+        h2 = hidden(pre[2], HALF, "h2", 28 * KIB)
 
-        m0 = rest(s0, CHUNK, "m0")
+        m0 = factor(h0, CHUNK, "m0")
         nc.vector.quantize_mx(out=w2_codes[:].bitcast(FP8X4), scales=w2_scales[:], in_=w2_bf[:])
-        z0 = weave(0, s0[:], m0[:])
-        m1 = rest(s1, CHUNK, "m1")
-        y0 = product(0, z0)
-        z1 = weave(1, s1[:], m1[:])
-        m2 = rest(s2, HALF, "m2")
-        y1 = product(1, z1)
-        kept = [tile([P, HALF], F32, f"kept{a}") for a in range(2)]
-        kept0 = dragged(kept[0][:], g0)
-        kept1 = dragged(kept[1][:], g1)
-        kick(0, y0, kept0)
-        put(0, CHUNK)
-        z2 = weave(2, s2[:, 0:CHUNK // RUN], m2[:, 0:CHUNK // RUN])
-        kick(1, y1, kept0)
-        put(CHUNK, CHUNK)
-        y2 = product(2, z2)
-        z3 = weave(3, s2[:, CHUNK // RUN:], m2[:, CHUNK // RUN:])
-        kick(2, y2, kept1)
-        put(2 * CHUNK, CHUNK)
-        y3 = product(3, z3)
-        kick(3, y3, kept1)
-        put(3 * CHUNK, CHUNK)
-
+        z0 = weave(0, h0[:], m0[:])
+        m1 = factor(h1, CHUNK, "m1")
+        y0 = second_product(0, z0)
+        kept0 = dragged(0, g0)
+        g1 = look_up(1, "mom_g0")
+        z1 = weave(1, h1[:], m1[:], 32 * KIB)
+        new0 = kick(0, y0, kept0)
+        put(0, new0)
+        y1 = second_product(1, z1)
+        m2 = factor(h2, HALF, "m2")
+        new1 = kick(1, y1, kept0, 34 * KIB)
+        put(1, new1)
+        z2 = weave(2, h2[:, :, 0:CHUNK], m2[:, :, 0:CHUNK])
+        kept1 = dragged(1, g1, "kept0")
+        y2 = second_product(2, z2)
+        z3 = weave(3, h2[:, :, CHUNK:], m2[:, :, CHUNK:], "mom_g0")
+        new2 = kick(2, y2, kept1)
+        put(2, new2)
+        y3 = second_product(3, z3)
+        new3 = kick(3, y3, kept1)
+        put(3, new3)
         nc.sync.dma_start(out=out, in_=window[:])

@@ -99,13 +99,11 @@ def tile_picked_yham_drag_p_kernel(
         nc.gpsimd.dma_start(out=top_t[:], in_=top.rearrange("(p t) o -> p (t o)", t=PACK))
         neg_top = tile([P, PACK], F32, "neg_top")
         drag_kick = tile([P, 1], F32, "drag_kick")
-        pos_top = tile([P, PACK], F32, "pos_top")
         twice_bias = tile([P, PACK], F32, "twice_bias")
         nc.gpsimd.tensor_scalar(twice_bias[:], bias_t[:], 2.0, 0.0, ALU.mult, ALU.add)
-        nc.gpsimd.tensor_scalar(pos_top[:], top_t[:], 4.0, 0.0, ALU.mult, ALU.add)
         nc.gpsimd.tensor_scalar(neg_top[:], top_t[:], -4.0, 0.0, ALU.mult, ALU.add)
         third_top = placed([P, 1], F32, "third_top", 34 * KIB)
-        nc.gpsimd.tensor_scalar(third_top[:], top_t[:, 2:3], 4.0, 0.0, ALU.mult, ALU.add)
+        nc.gpsimd.tensor_scalar(third_top[:], top_t[:, 2:3], -4.0, 0.0, ALU.mult, ALU.add)
 
         w1_codes = [tile([P, H], U32, f"w1_c{g}") for g in range(PASSES)]
         w1_scales = [tile([P, H], U8, f"w1_s{g}") for g in range(PASSES)]
@@ -172,8 +170,8 @@ def tile_picked_yham_drag_p_kernel(
         def factor(s, width, name, where=None):
             m = scratch([P, PACK, width], F32, name, where)
             for t in range(PACK):
-                plus = third_top[:] if width == HALF and t == 2 else pos_top[:, t:t + 1]
-                nc.vector.tensor_scalar(m[:, t, :], s[:, t, :], neg_top[:, t:t + 1], plus, ALU.mult, ALU.add)
+                times = third_top[:] if width == HALF and t == 2 else neg_top[:, t:t + 1]
+                nc.vector.tensor_scalar(m[:, t, :], s[:, t, :], -1.0, times, ALU.add, ALU.mult)
             return m
 
         def weave(c, s, m, where=None):

@@ -26,6 +26,7 @@ PAIRS = 2
 PAIR = PACK // PAIRS
 HALF = 256
 CHUNK = 128
+RUN = 4
 KICK = 0.4
 KIB = 1024
 
@@ -162,30 +163,31 @@ def tile_picked_yham_drag_p_kernel(
             return placed(shape, dtype, name, where) if isinstance(where, int) else tile(shape, dtype, name, where)
 
         def hidden(sums, width, name, where=None):
-            s = scratch([P, PACK, width], F32, name, where)
+            s = scratch([P, width // RUN, PACK, RUN], F32, name, where)
             for t in range(PACK):
-                nc.scalar.activation(s[:, t, :], sums[t], ACT.Sigmoid, bias=twice_bias[:, t:t + 1], scale=2.0)
+                nc.scalar.activation(s[:, :, t, :], sums[t].rearrange("p (c i) -> p c i", i=RUN), ACT.Sigmoid,
+                                     bias=twice_bias[:, t:t + 1], scale=2.0)
             return s
 
         def factor(s, width, name, where=None):
-            m = scratch([P, PACK, width], F32, name, where)
+            m = scratch([P, width // RUN, PACK, RUN], F32, name, where)
             for t in range(PACK):
                 times = third_top[:] if width == HALF and t == 2 else neg_top[:, t:t + 1]
-                nc.vector.tensor_scalar(m[:, t, :], s[:, t, :], -1.0, times, ALU.add, ALU.mult)
+                nc.vector.tensor_scalar(m[:, :, t, :], s[:, :, t, :], -1.0, times, ALU.add, ALU.mult)
             return m
 
         def weave(c, s, m, where=None):
-            z_bf = scratch([P, CHUNK, PACK], BF16, f"z_b{c}", where)
-            nc.vector.tensor_tensor(z_bf[:].rearrange("p (c i) t -> p c t i", i=PAIR),
-                                    s.rearrange("p t (c i) -> p c t i", i=PAIR),
-                                    m.rearrange("p t (c i) -> p c t i", i=PAIR), ALU.mult)
+            z_bf = scratch([P, RUN, CHUNK // RUN, PACK], BF16, f"z_b{c}", where)
+            nc.vector.tensor_tensor(z_bf[:].rearrange("p i c (u v) -> p (c u) i v", v=PAIR),
+                                    s.rearrange("p c (u v) i -> p (c u) i v", v=PAIR),
+                                    m.rearrange("p c (u v) i -> p (c u) i v", v=PAIR), ALU.mult)
             return z_bf
 
         def second_product(c, z_bf, tag=None):
             z_codes = tile([P, CHUNK], U32, f"z_c{c}", tag)
             z_scales = tile([P, CHUNK], U8, f"z_s{c}")
             nc.vector.quantize_mx(out=z_codes[:].bitcast(FP8X4), scales=z_scales[:],
-                                  in_=z_bf[:].rearrange("p c t -> p (c t)"))
+                                  in_=z_bf[:].rearrange("p i c t -> p (i c t)"))
             y = ps.tile([P, CHUNK], F32, name=f"y{c}", tag=f"bank0_{c}")
             nc.tensor.matmul_mx(out=y[:], lhsT=w2_codes[:].bitcast(FP8X4), lhsT_scale=w2_scales[:],
                                 rhs=z_codes[:].bitcast(FP8X4), rhs_scale=z_scales[:], start=True, stop=True)
@@ -204,7 +206,10 @@ def tile_picked_yham_drag_p_kernel(
         def kick(c, y, kept, where=None):
             new = scratch([P, CHUNK], F32, f"new{c}", where)
             first = c * CHUNK % HALF
-            nc.vector.scalar_tensor_tensor(new[:], y[:], drag_kick[:], kept[:, first:first + CHUNK], ALU.mult, ALU.add)
+            nc.vector.scalar_tensor_tensor(new[:].rearrange("p (c i) -> p c i", i=RUN),
+                                           y[:].rearrange("p (i c) -> p c i", i=RUN), drag_kick[:],
+                                           kept[:, first:first + CHUNK].rearrange("p (c i) -> p c i", i=RUN),
+                                           ALU.mult, ALU.add)
             return new
 
         def put(c, new):
@@ -229,10 +234,10 @@ def tile_picked_yham_drag_p_kernel(
         m2 = factor(h2, HALF, "m2")
         new1 = kick(1, y1, kept0, 34 * KIB)
         put(1, new1)
-        z2 = weave(2, h2[:, :, 0:CHUNK], m2[:, :, 0:CHUNK])
+        z2 = weave(2, h2[:, 0:CHUNK // RUN], m2[:, 0:CHUNK // RUN])
         kept1 = dragged(1, g1, "kept0")
         y2 = second_product(2, z2)
-        z3 = weave(3, h2[:, :, CHUNK:], m2[:, :, CHUNK:], "mom_g0")
+        z3 = weave(3, h2[:, CHUNK // RUN:], m2[:, CHUNK // RUN:], "mom_g0")
         new2 = kick(2, y2, kept1)
         put(2, new2)
         y3 = second_product(3, z3)

@@ -78,10 +78,6 @@ def tile_picked_yham_drag_p_kernel(
                 nc.sync.dma_start(out=picked_scales[g][QUADRANT * q:QUADRANT * q + SCALE_ROWS, :].bitcast(I32),
                                   in_=picked_rows[first:QUADRANT * (q + 1):PASSES * SCALE_ROWS, :].bitcast(I32))
 
-        warm_in = tile([P, 1], F32, "warm_in")
-        warm_out = tile([P, 1], F32, "warm_out")
-        nc.gpsimd.memset(warm_in[:], 0.0)
-        nc.scalar.activation(warm_out[:], warm_in[:], ACT.Sigmoid)
         nc.vector.memset(x_scale_t[:].bitcast(I32), 0)
         for g in range(PASSES):
             nc.vector.memset(picked_scales[g][:].bitcast(I32), 0)
@@ -100,11 +96,9 @@ def tile_picked_yham_drag_p_kernel(
         nc.gpsimd.dma_start(out=top_t[:], in_=top.rearrange("(p t) o -> p (t o)", t=PACK))
         neg_top = tile([P, PACK], F32, "neg_top")
         drag_kick = tile([P, 1], F32, "drag_kick")
-        twice_bias = tile([P, PACK], F32, "twice_bias")
-        nc.gpsimd.tensor_scalar(twice_bias[:], bias_t[:], 2.0, 0.0, ALU.mult, ALU.add)
-        nc.gpsimd.tensor_scalar(neg_top[:], top_t[:], -4.0, 0.0, ALU.mult, ALU.add)
-        third_top = placed([P, 1], F32, "third_top", 34 * KIB)
-        nc.gpsimd.tensor_scalar(third_top[:], top_t[:, 2:3], -4.0, 0.0, ALU.mult, ALU.add)
+        nc.gpsimd.tensor_scalar(neg_top[:], top_t[:], -1.0, 0.0, ALU.mult, ALU.add)
+        last_top = placed([P, 1], F32, "last_top", 34 * KIB)
+        nc.gpsimd.tensor_scalar(last_top[:], top_t[:, 3:4], -1.0, 0.0, ALU.mult, ALU.add)
 
         w1_codes = [tile([P, H], U32, f"w1_c{g}") for g in range(PASSES)]
         w1_scales = [tile([P, H], U8, f"w1_s{g}") for g in range(PASSES)]
@@ -158,6 +152,8 @@ def tile_picked_yham_drag_p_kernel(
         nc.gpsimd.tensor_scalar(w2_bf[:].rearrange("p (n j) -> p n j", j=PACK), w2_raw[:].rearrange("p j n -> p n j"),
                                 1.0, 0.0, ALU.mult, ALU.add)
         nc.gpsimd.tensor_scalar(drag_kick[:], drag_t[:, 0:1], -KICK, 0.0, ALU.mult, ALU.add)
+        second_kick = placed([P, 1], F32, "second_kick", 35 * KIB)
+        nc.gpsimd.tensor_scalar(second_kick[:], drag_kick[:], 1.0, 0.0, ALU.mult, ALU.add)
 
         def scratch(shape, dtype, name, where):
             return placed(shape, dtype, name, where) if isinstance(where, int) else tile(shape, dtype, name, where)
@@ -165,22 +161,26 @@ def tile_picked_yham_drag_p_kernel(
         def hidden(sums, width, name, where=None):
             s = scratch([P, width // RUN, PACK, RUN], F32, name, where)
             for t in range(PACK):
-                nc.scalar.activation(s[:, :, t, :], sums[t].rearrange("p (c i) -> p c i", i=RUN), ACT.Sigmoid,
-                                     bias=twice_bias[:, t:t + 1], scale=2.0)
+                nc.scalar.activation(s[:, :, t, :], sums[t].rearrange("p (c i) -> p c i", i=RUN), ACT.Tanh,
+                                     bias=bias_t[:, t:t + 1])
             return s
 
-        def factor(s, width, name, where=None):
-            m = scratch([P, width // RUN, PACK, RUN], F32, name, where)
+        def factor(c, h):
+            m = tile([P, CHUNK // RUN, PACK, RUN], F32, f"m{c}")
             for t in range(PACK):
-                times = third_top[:] if width == HALF and t == 2 else neg_top[:, t:t + 1]
-                nc.vector.tensor_scalar(m[:, :, t, :], s[:, :, t, :], -1.0, times, ALU.add, ALU.mult)
+                if c == 3:
+                    nc.scalar.activation(m[:, :, t, :], h[:, :, t, :], ACT.Identity, bias=top_t[:, t:t + 1],
+                                         scale=neg_top[:, t:t + 1])
+                else:
+                    times = last_top[:] if c == 2 and t == 3 else neg_top[:, t:t + 1]
+                    nc.vector.tensor_scalar(m[:, :, t, :], h[:, :, t, :], -1.0, times, ALU.add, ALU.mult)
             return m
 
-        def weave(c, s, m, where=None):
+        def weave(c, h, m, where=None):
             z_bf = scratch([P, RUN, CHUNK // RUN, PACK], BF16, f"z_b{c}", where)
-            nc.vector.tensor_tensor(z_bf[:].rearrange("p i c (u v) -> p (c u) i v", v=PAIR),
-                                    s.rearrange("p c (u v) i -> p (c u) i v", v=PAIR),
-                                    m.rearrange("p c (u v) i -> p (c u) i v", v=PAIR), ALU.mult)
+            nc.vector.scalar_tensor_tensor(z_bf[:].rearrange("p i c t -> p (c t) i"),
+                                           h.rearrange("p c t i -> p (c t) i"), 1.0,
+                                           m.rearrange("p c t i -> p (c t) i"), ALU.add, ALU.mult)
             return z_bf
 
         def second_product(c, z_bf, tag=None):
@@ -193,23 +193,22 @@ def tile_picked_yham_drag_p_kernel(
                                 rhs=z_codes[:].bitcast(FP8X4), rhs_scale=z_scales[:], start=True, stop=True)
             return y
 
-        def look_up(a, tag=None):
-            picked = tile([P, HALF], F32, f"mom_g{a}", tag)
-            nc.scalar.activation(picked[:], table[:].indirect(entries(slot_t, a * HALF, HALF)), ACT.Copy)
+        def look_up(first, count, tag=None):
+            picked = tile([P, count], F32, f"mom_g{first}", tag)
+            nc.scalar.activation(picked[:], table[:].indirect(entries(slot_t, first, count)), ACT.Copy)
             return picked
 
-        def dragged(a, picked, tag=None):
-            kept = tile([P, HALF], F32, f"kept{a}", tag)
+        def dragged(name, picked, count, tag=None):
+            kept = tile([P, count], F32, name, tag)
             nc.vector.tensor_scalar(kept[:], picked[:], drag_kick[:], -1.0 / KICK, ALU.mult, ALU.mult)
             return kept
 
         def kick(c, y, kept, where=None):
             new = scratch([P, CHUNK], F32, f"new{c}", where)
-            first = c * CHUNK % HALF
             nc.vector.scalar_tensor_tensor(new[:].rearrange("p (c i) -> p c i", i=RUN),
-                                           y[:].rearrange("p (i c) -> p c i", i=RUN), drag_kick[:],
-                                           kept[:, first:first + CHUNK].rearrange("p (c i) -> p c i", i=RUN),
-                                           ALU.mult, ALU.add)
+                                           y[:].rearrange("p (i c) -> p c i", i=RUN),
+                                           second_kick[:] if c == 1 else drag_kick[:],
+                                           kept.rearrange("p (c i) -> p c i", i=RUN), ALU.mult, ALU.add)
             return new
 
         def put(c, new):
@@ -217,30 +216,34 @@ def tile_picked_yham_drag_p_kernel(
 
         h0 = hidden(pre[0], CHUNK, "h0")
         h1 = hidden(pre[1], CHUNK, "h1")
-        g0 = look_up(0)
-        h2 = hidden(pre[2], HALF, "h2", 28 * KIB)
+        g0 = look_up(0, CHUNK)
+        h23 = hidden(pre[2], HALF, "h23", 28 * KIB)
+        h2, h3 = h23[:, 0:CHUNK // RUN], h23[:, CHUNK // RUN:]
 
-        m0 = factor(h0, CHUNK, "m0")
+        m0 = factor(0, h0[:])
         nc.vector.quantize_mx(out=w2_codes[:].bitcast(FP8X4), scales=w2_scales[:], in_=w2_bf[:])
         z0 = weave(0, h0[:], m0[:])
-        m1 = factor(h1, CHUNK, "m1")
+        m1 = factor(1, h1[:])
         y0 = second_product(0, z0)
-        kept0 = dragged(0, g0)
-        g1 = look_up(1, "mom_g0")
+        kept0 = dragged("kept0", g0, CHUNK)
+        g12 = look_up(CHUNK, HALF, "mom_g0")
+        m3 = factor(3, h3)
         z1 = weave(1, h1[:], m1[:], 32 * KIB)
-        new0 = kick(0, y0, kept0)
+        new0 = kick(0, y0, kept0[:])
         put(0, new0)
+        g3 = look_up(3 * CHUNK, CHUNK)
         y1 = second_product(1, z1)
-        m2 = factor(h2, HALF, "m2")
-        new1 = kick(1, y1, kept0, 34 * KIB)
+        m2 = factor(2, h2)
+        kept12 = dragged("kept12", g12, HALF)
+        z2 = weave(2, h2, m2[:])
+        new1 = kick(1, y1, kept12[:, 0:CHUNK], 34 * KIB)
         put(1, new1)
-        z2 = weave(2, h2[:, 0:CHUNK // RUN], m2[:, 0:CHUNK // RUN])
-        kept1 = dragged(1, g1, "kept0")
         y2 = second_product(2, z2)
-        z3 = weave(3, h2[:, CHUNK // RUN:], m2[:, CHUNK // RUN:], "mom_g0")
-        new2 = kick(2, y2, kept1)
+        z3 = weave(3, h3, m3[:], 35 * KIB)
+        new2 = kick(2, y2, kept12[:, CHUNK:])
         put(2, new2)
         y3 = second_product(3, z3)
-        new3 = kick(3, y3, kept1)
+        kept3 = dragged("kept3", g3, CHUNK, "m3")
+        new3 = kick(3, y3, kept3[:])
         put(3, new3)
         nc.sync.dma_start(out=out, in_=window[:])

@@ -27,6 +27,7 @@ PAIR = PACK // PAIRS
 HALF = 256
 CHUNK = 128
 RUN = 4
+HELPED = 40
 KICK = 0.4
 KIB = 1024
 
@@ -109,14 +110,17 @@ def tile_picked_yham_drag_p_kernel(
                      else tile([P, PAIR * P * PACK], BF16, f"w1_b{g}_{u}") for u in range(PAIRS)]
             dst = [w1_bf[u][:].rearrange("p (v m j) -> p m v j", v=PAIR, j=PACK) for u in range(PAIRS)]
             nc.vector.tensor_copy(dst[0], src[:, 0])
-            nc.scalar.copy(dst[1], src[:, 1])
+            helped = HELPED * g
+            if helped:
+                nc.vector.tensor_copy(dst[1][:, 0:helped], src[:, 1, 0:helped])
+            nc.scalar.copy(dst[1][:, helped:], src[:, 1, helped:])
             for u in range(PAIRS):
                 cols = slice(u * PAIR * P, (u + 1) * PAIR * P)
                 nc.vector.quantize_mx(out=w1_codes[g][:, cols].bitcast(FP8X4), scales=w1_scales[g][:, cols],
                                       in_=w1_bf[u][:])
 
         picked_words = [tile([P, S], U32, f"gx{g}") for g in range(PASSES)]
-        pieces = ((0, CHUNK, 1), (CHUNK, CHUNK, PACK), (HALF, HALF, PAIR))
+        pieces = ((0, CHUNK, 1), (CHUNK, CHUNK, PAIR), (HALF, HALF, PAIR))
         banks = [[ps.tile([P, shared, count], F32, name=f"pre{a}_{b}", tag=f"bank{a}_{b}")
                   for b in range(PACK // shared)] for a, (first, count, shared) in enumerate(pieces)]
         pre = [[banks[a][t // shared][:, t % shared, :] for t in range(PACK)]
@@ -152,8 +156,6 @@ def tile_picked_yham_drag_p_kernel(
         nc.gpsimd.tensor_scalar(w2_bf[:].rearrange("p (n j) -> p n j", j=PACK), w2_raw[:].rearrange("p j n -> p n j"),
                                 1.0, 0.0, ALU.mult, ALU.add)
         nc.gpsimd.tensor_scalar(drag_kick[:], drag_t[:, 0:1], -KICK, 0.0, ALU.mult, ALU.add)
-        second_kick = placed([P, 1], F32, "second_kick", 35 * KIB)
-        nc.gpsimd.tensor_scalar(second_kick[:], drag_kick[:], 1.0, 0.0, ALU.mult, ALU.add)
 
         def scratch(shape, dtype, name, where):
             return placed(shape, dtype, name, where) if isinstance(where, int) else tile(shape, dtype, name, where)
@@ -176,9 +178,11 @@ def tile_picked_yham_drag_p_kernel(
                     nc.vector.tensor_scalar(m[:, :, t, :], h[:, :, t, :], -1.0, times, ALU.add, ALU.mult)
             return m
 
-        def weave(c, h, m, where=None):
-            z_bf = scratch([P, RUN, CHUNK // RUN, PACK], BF16, f"z_b{c}", where)
-            nc.vector.scalar_tensor_tensor(z_bf[:].rearrange("p i c t -> p (c t) i"),
+        def z_tile(c, where=None):
+            return scratch([P, CHUNK * PACK], BF16, f"z_b{c}", where)[:]
+
+        def weave(z_bf, h, m):
+            nc.vector.scalar_tensor_tensor(z_bf.rearrange("p (i ct) -> p ct i", i=RUN),
                                            h.rearrange("p c t i -> p (c t) i"), 1.0,
                                            m.rearrange("p c t i -> p (c t) i"), ALU.add, ALU.mult)
             return z_bf
@@ -187,7 +191,7 @@ def tile_picked_yham_drag_p_kernel(
             z_codes = tile([P, CHUNK], U32, f"z_c{c}", tag)
             z_scales = tile([P, CHUNK], U8, f"z_s{c}")
             nc.vector.quantize_mx(out=z_codes[:].bitcast(FP8X4), scales=z_scales[:],
-                                  in_=z_bf[:].rearrange("p i c t -> p (i c t)"))
+                                  in_=z_bf)
             y = ps.tile([P, CHUNK], F32, name=f"y{c}", tag=f"bank0_{c}")
             nc.tensor.matmul_mx(out=y[:], lhsT=w2_codes[:].bitcast(FP8X4), lhsT_scale=w2_scales[:],
                                 rhs=z_codes[:].bitcast(FP8X4), rhs_scale=z_scales[:], start=True, stop=True)
@@ -198,16 +202,14 @@ def tile_picked_yham_drag_p_kernel(
             nc.scalar.activation(picked[:], table[:].indirect(entries(slot_t, first, count)), ACT.Copy)
             return picked
 
-        def dragged(name, picked, count, tag=None):
-            kept = tile([P, count], F32, name, tag)
-            nc.vector.tensor_scalar(kept[:], picked[:], drag_kick[:], -1.0 / KICK, ALU.mult, ALU.mult)
+        def dragged(kept, picked):
+            nc.vector.tensor_scalar(kept, picked[:], drag_kick[:], -1.0 / KICK, ALU.mult, ALU.mult)
             return kept
 
         def kick(c, y, kept, where=None):
             new = scratch([P, CHUNK], F32, f"new{c}", where)
             nc.vector.scalar_tensor_tensor(new[:].rearrange("p (c i) -> p c i", i=RUN),
-                                           y[:].rearrange("p (i c) -> p c i", i=RUN),
-                                           second_kick[:] if c == 1 else drag_kick[:],
+                                           y[:].rearrange("p (i c) -> p c i", i=RUN), drag_kick[:],
                                            kept.rearrange("p (c i) -> p c i", i=RUN), ALU.mult, ALU.add)
             return new
 
@@ -222,28 +224,29 @@ def tile_picked_yham_drag_p_kernel(
 
         m0 = factor(0, h0[:])
         nc.vector.quantize_mx(out=w2_codes[:].bitcast(FP8X4), scales=w2_scales[:], in_=w2_bf[:])
-        z0 = weave(0, h0[:], m0[:])
+        z0 = weave(z_tile(0), h0[:], m0[:])
         m1 = factor(1, h1[:])
         y0 = second_product(0, z0)
-        kept0 = dragged("kept0", g0, CHUNK)
+        kept0 = dragged(tile([P, CHUNK], F32, "kept0")[:], g0)
         g12 = look_up(CHUNK, HALF, "mom_g0")
         m3 = factor(3, h3)
-        z1 = weave(1, h1[:], m1[:], 32 * KIB)
-        new0 = kick(0, y0, kept0[:])
+        z1 = weave(z_tile(1, 32 * KIB), h1[:], m1[:])
+        new0 = kick(0, y0, kept0)
         put(0, new0)
         g3 = look_up(3 * CHUNK, CHUNK)
         y1 = second_product(1, z1)
         m2 = factor(2, h2)
-        kept12 = dragged("kept12", g12, HALF)
-        z2 = weave(2, h2, m2[:])
+        shared = tile([P, 3 * CHUNK], F32, "shared")
+        kept12 = dragged(shared[:, CHUNK:], g12)
+        z2 = weave(z_tile(2), h2, m2[:])
         new1 = kick(1, y1, kept12[:, 0:CHUNK], 34 * KIB)
         put(1, new1)
         y2 = second_product(2, z2)
-        z3 = weave(3, h3, m3[:], 35 * KIB)
+        z3 = weave(shared[:, 0:2 * CHUNK].bitcast(BF16), h3, m3[:])
         new2 = kick(2, y2, kept12[:, CHUNK:])
         put(2, new2)
         y3 = second_product(3, z3)
-        kept3 = dragged("kept3", g3, CHUNK, "m3")
-        new3 = kick(3, y3, kept3[:])
+        kept3 = dragged(tile([P, CHUNK], F32, "kept3", "m3")[:], g3)
+        new3 = kick(3, y3, kept3)
         put(3, new3)
         nc.sync.dma_start(out=out, in_=window[:])

@@ -24,12 +24,24 @@ SCALE_ROWS = 4
 LIST_ROWS = 16
 PAIRS = 2
 PAIR = PACK // PAIRS
-HALF = 256
 CHUNK = 128
+HALF = 2 * CHUNK
 RUN = 4
 HELPED = 40
 KICK = 0.4
+
 KIB = 1024
+OVERLAP = 64
+LAST_WORDS_AT = 0
+SCALE_STAGE_AT = 8 * KIB - OVERLAP
+FIRST_ROUNDED_AT = SCALE_STAGE_AT + T - OVERLAP
+FIRST_WORDS_AT = 12 * KIB
+FIRST_W1_AT = 20 * KIB
+DRAG_AT = 32 * KIB - OVERLAP
+LAST_HIDDEN_AT = DRAG_AT + OVERLAP - 2 * KIB
+SECOND_SCALES_AT = DRAG_AT + OVERLAP
+THIRD_FACTOR_AT = SECOND_SCALES_AT + CHUNK
+LAST_TOP_AT = 35 * KIB
 
 
 def tile_picked_yham_drag_p_kernel(
@@ -41,29 +53,28 @@ def tile_picked_yham_drag_p_kernel(
         ps = ctx.enter_context(tc.psum_pool(name="ps", bufs=1))
         laid = ctx.enter_context(tc.tile_pool(name="laid", bufs=1))
 
-        def placed(shape, dtype, name, offset):
-            return laid.tile(shape, dtype, name=name, align_bytes=64, offset=offset)
-
-        def tile(shape, dtype, name, tag=None):
-            return sb.tile(shape, dtype, name=name, tag=tag or name, align_bytes=64)
+        def tile(shape, dtype, name, at=None, tag=None):
+            if at is None:
+                return sb.tile(shape, dtype, name=name, tag=tag or name, align_bytes=64)
+            return laid.tile(shape, dtype, name=name, align_bytes=64, offset=at)
 
         def entries(list_tile, first, count):
             return list_tile[:, first // LIST_ROWS:(first + count) // LIST_ROWS]
 
         offs_t = sb.tile([P, S // LIST_ROWS], U16, name="offs_t")
         slot_t = sb.tile([P, S // LIST_ROWS], U16, name="slot_t")
-        x_word_t = [placed([P, T], U32, "xw0", 12 * KIB), placed([P, T], U32, "xw1", 0)]
-        x_scale_t = placed([P, T], U8, "xs", 8 * KIB - 64)
-        w1_first = placed([P, PAIR * P * PACK], BF16, "w1_first", 10 * KIB - 128)
-        table = placed([P, U], F32, "table", 12 * KIB)
-        window = placed([P, U], F32, "window", 16 * KIB)
-        w1_raw = [placed([P, PACK, H], F32, "w1_raw0", 20 * KIB), tile([P, PACK, H], F32, "w1_raw1")]
-        w2_raw = placed([P, PACK, N], F32, "w2_raw", 20 * KIB)
+        x_word_t = [tile([P, T], U32, "xw0", FIRST_WORDS_AT), tile([P, T], U32, "xw1", LAST_WORDS_AT)]
+        x_scale_t = tile([P, T], U8, "xs", SCALE_STAGE_AT)
+        w1_first = tile([P, PAIR * P * PACK], BF16, "w1_first", FIRST_ROUNDED_AT)
+        table = tile([P, U], F32, "table", FIRST_WORDS_AT)
+        window = tile([P, U], F32, "window", FIRST_WORDS_AT + 4 * U)
+        w1_raw = [tile([P, PACK, H], F32, "w1_raw0", FIRST_W1_AT), tile([P, PACK, H], F32, "w1_raw1")]
+        w2_raw = tile([P, PACK, N], F32, "w2_raw", FIRST_W1_AT)
         picked_rows = tile([P, S], U8, "picked_rows")
         picked_scales = [tile([P, S], U8, f"gs{g}") for g in range(PASSES)]
         bias_t = tile([P, PACK], F32, "bias_t")
         top_t = tile([P, PACK], F32, "top_t")
-        drag_t = placed([P, 32], F32, "drag_t", 32 * KIB - 64)
+        drag_t = tile([P, OVERLAP], F32, "drag_t", DRAG_AT)
 
         def load_w1(g):
             rows = w1[g * K_PASS:(g + 1) * K_PASS, :]
@@ -98,19 +109,18 @@ def tile_picked_yham_drag_p_kernel(
         neg_top = tile([P, PACK], F32, "neg_top")
         drag_kick = tile([P, 1], F32, "drag_kick")
         nc.gpsimd.tensor_scalar(neg_top[:], top_t[:], -1.0, 0.0, ALU.mult, ALU.add)
-        last_top = placed([P, 1], F32, "last_top", 34 * KIB)
-        nc.gpsimd.tensor_scalar(last_top[:], top_t[:, 3:4], -1.0, 0.0, ALU.mult, ALU.add)
+        last_top = tile([P, 1], F32, "last_top", LAST_TOP_AT)
+        nc.gpsimd.tensor_scalar(last_top[:], top_t[:, PACK - 1:PACK], -1.0, 0.0, ALU.mult, ALU.add)
 
         w1_codes = [tile([P, H], U32, f"w1_c{g}") for g in range(PASSES)]
         w1_scales = [tile([P, H], U8, f"w1_s{g}") for g in range(PASSES)]
 
-        def quantise_w1(g):
+        def quantise_w1(g, helped):
             src = w1_raw[g][:].rearrange("p j (m u v) -> p u m v j", u=PAIRS, v=PAIR)
             w1_bf = [w1_first if g == 0 and u == 0
                      else tile([P, PAIR * P * PACK], BF16, f"w1_b{g}_{u}") for u in range(PAIRS)]
             dst = [w1_bf[u][:].rearrange("p (v m j) -> p m v j", v=PAIR, j=PACK) for u in range(PAIRS)]
             nc.vector.tensor_copy(dst[0], src[:, 0])
-            helped = HELPED * g
             if helped:
                 nc.vector.tensor_copy(dst[1][:, 0:helped], src[:, 1, 0:helped])
             nc.scalar.copy(dst[1][:, helped:], src[:, 1, helped:])
@@ -120,34 +130,35 @@ def tile_picked_yham_drag_p_kernel(
                                       in_=w1_bf[u][:])
 
         picked_words = [tile([P, S], U32, f"gx{g}") for g in range(PASSES)]
-        pieces = ((0, CHUNK, 1), (CHUNK, CHUNK, PAIR), (HALF, HALF, PAIR))
-        banks = [[ps.tile([P, shared, count], F32, name=f"pre{a}_{b}", tag=f"bank{a}_{b}")
-                  for b in range(PACK // shared)] for a, (first, count, shared) in enumerate(pieces)]
-        pre = [[banks[a][t // shared][:, t % shared, :] for t in range(PACK)]
-               for a, (first, count, shared) in enumerate(pieces)]
+        shared_by = (1, PAIR, PACK, PACK)
+        banks = [[ps.tile([P, shared, CHUNK], F32, name=f"pre{c}_{b}", tag=f"bank{c}_{b}")
+                  for b in range(PACK // shared)] for c, shared in enumerate(shared_by)]
+        pre = [[banks[c][t // shared][:, t % shared, :] for t in range(PACK)] for c, shared in enumerate(shared_by)]
 
         def first_product(g):
-            for a, (first, count, shared) in enumerate(pieces):
+            for first, count in ((0, CHUNK), (CHUNK, CHUNK), (HALF, HALF)):
                 nc.vector.tensor_copy(picked_words[g][:, first:first + count],
                                       x_word_t[g][:].indirect(entries(offs_t, first, count)))
-                for t in range(PACK):
-                    nc.tensor.matmul_mx(
-                        out=pre[a][t],
-                        lhsT=w1_codes[g][:, t * P:(t + 1) * P].bitcast(FP8X4),
-                        lhsT_scale=w1_scales[g][:, t * P:(t + 1) * P],
-                        rhs=picked_words[g][:, first:first + count].bitcast(FP8X4),
-                        rhs_scale=picked_scales[g][:, first:first + count],
-                        start=g == 0 and t % shared == 0,
-                        stop=g == PASSES - 1 and t % shared == shared - 1)
+                for c in range(first // CHUNK, (first + count) // CHUNK):
+                    tokens = slice(c * CHUNK, (c + 1) * CHUNK)
+                    for t in range(PACK):
+                        nc.tensor.matmul_mx(
+                            out=pre[c][t],
+                            lhsT=w1_codes[g][:, t * P:(t + 1) * P].bitcast(FP8X4),
+                            lhsT_scale=w1_scales[g][:, t * P:(t + 1) * P],
+                            rhs=picked_words[g][:, tokens].bitcast(FP8X4),
+                            rhs_scale=picked_scales[g][:, tokens],
+                            start=g == 0 and t % shared_by[c] == 0,
+                            stop=g == PASSES - 1 and t % shared_by[c] == shared_by[c] - 1)
 
-        quantise_w1(0)
+        quantise_w1(0, 0)
         first_product(0)
         nc.sync.dma_start(out=w2_raw[:], in_=w2.rearrange("(p j) n -> p j n", j=PACK))
         nc.sync.dma_start(slot_t[:], slot)
         nc.sync.dma_start(out=table[:], in_=mom)
         nc.sync.dma_start(out=drag_t[:, 0:1], in_=drag)
         nc.sync.dma_start(out=window[:], in_=mom)
-        quantise_w1(1)
+        quantise_w1(1, HELPED)
         first_product(1)
 
         w2_bf = tile([P, N * PACK], BF16, "w2_b")
@@ -157,48 +168,44 @@ def tile_picked_yham_drag_p_kernel(
                                 1.0, 0.0, ALU.mult, ALU.add)
         nc.gpsimd.tensor_scalar(drag_kick[:], drag_t[:, 0:1], -KICK, 0.0, ALU.mult, ALU.add)
 
-        def scratch(shape, dtype, name, where):
-            return placed(shape, dtype, name, where) if isinstance(where, int) else tile(shape, dtype, name, where)
+        by_runs = [P, CHUNK // RUN, PACK, RUN]
 
-        def hidden(sums, width, name, where=None):
-            s = scratch([P, width // RUN, PACK, RUN], F32, name, where)
+        def hidden(c, at=None):
+            h = tile(by_runs, F32, f"h{c}", at)
             for t in range(PACK):
-                nc.scalar.activation(s[:, :, t, :], sums[t].rearrange("p (c i) -> p c i", i=RUN), ACT.Tanh,
+                nc.scalar.activation(h[:, :, t, :], pre[c][t].rearrange("p (c i) -> p c i", i=RUN), ACT.Tanh,
                                      bias=bias_t[:, t:t + 1])
-            return s
+            return h
 
-        def factor(c, h):
-            m = tile([P, CHUNK // RUN, PACK, RUN], F32, f"m{c}")
+        def factor(m, h, t, minus_top):
+            nc.vector.tensor_scalar(m[:, :, t, :], h[:, :, t, :], -1.0, minus_top, ALU.add, ALU.mult)
+
+        def whole_factor(c, h):
+            m = tile(by_runs, F32, f"m{c}")
             for t in range(PACK):
-                if c == 3:
-                    nc.scalar.activation(m[:, :, t, :], h[:, :, t, :], ACT.Identity, bias=top_t[:, t:t + 1],
-                                         scale=neg_top[:, t:t + 1])
-                else:
-                    times = last_top[:] if c == 2 and t == 3 else neg_top[:, t:t + 1]
-                    nc.vector.tensor_scalar(m[:, :, t, :], h[:, :, t, :], -1.0, times, ALU.add, ALU.mult)
+                factor(m, h, t, neg_top[:, t:t + 1])
             return m
 
-        def z_tile(c, where=None):
-            return scratch([P, CHUNK * PACK], BF16, f"z_b{c}", where)[:]
+        def z_tile(c):
+            return tile([P, CHUNK * PACK], BF16, f"z_b{c}")[:]
 
         def weave(z_bf, h, m):
             nc.vector.scalar_tensor_tensor(z_bf.rearrange("p (i ct) -> p ct i", i=RUN),
-                                           h.rearrange("p c t i -> p (c t) i"), 1.0,
-                                           m.rearrange("p c t i -> p (c t) i"), ALU.add, ALU.mult)
+                                           h[:].rearrange("p c t i -> p (c t) i"), 1.0,
+                                           m[:].rearrange("p c t i -> p (c t) i"), ALU.add, ALU.mult)
             return z_bf
 
-        def second_product(c, z_bf, tag=None):
-            z_codes = tile([P, CHUNK], U32, f"z_c{c}", tag)
-            z_scales = tile([P, CHUNK], U8, f"z_s{c}")
-            nc.vector.quantize_mx(out=z_codes[:].bitcast(FP8X4), scales=z_scales[:],
-                                  in_=z_bf)
+        def second_product(c, z_bf, scales_at=None):
+            z_codes = tile([P, CHUNK], U32, f"z_c{c}")
+            z_scales = tile([P, CHUNK], U8, f"z_s{c}", scales_at)
+            nc.vector.quantize_mx(out=z_codes[:].bitcast(FP8X4), scales=z_scales[:], in_=z_bf)
             y = ps.tile([P, CHUNK], F32, name=f"y{c}", tag=f"bank0_{c}")
             nc.tensor.matmul_mx(out=y[:], lhsT=w2_codes[:].bitcast(FP8X4), lhsT_scale=w2_scales[:],
                                 rhs=z_codes[:].bitcast(FP8X4), rhs_scale=z_scales[:], start=True, stop=True)
             return y
 
-        def look_up(first, count, tag=None):
-            picked = tile([P, count], F32, f"mom_g{first}", tag)
+        def look_up(first, count):
+            picked = tile([P, count], F32, f"mom_g{first}")
             nc.scalar.activation(picked[:], table[:].indirect(entries(slot_t, first, count)), ACT.Copy)
             return picked
 
@@ -206,8 +213,8 @@ def tile_picked_yham_drag_p_kernel(
             nc.vector.tensor_scalar(kept, picked[:], drag_kick[:], -1.0 / KICK, ALU.mult, ALU.mult)
             return kept
 
-        def kick(c, y, kept, where=None):
-            new = scratch([P, CHUNK], F32, f"new{c}", where)
+        def kick(c, y, kept, at=None):
+            new = tile([P, CHUNK], F32, f"new{c}", at)
             nc.vector.scalar_tensor_tensor(new[:].rearrange("p (c i) -> p c i", i=RUN),
                                            y[:].rearrange("p (i c) -> p c i", i=RUN), drag_kick[:],
                                            kept.rearrange("p (c i) -> p c i", i=RUN), ALU.mult, ALU.add)
@@ -216,37 +223,40 @@ def tile_picked_yham_drag_p_kernel(
         def put(c, new):
             nc.scalar.activation(window[:].indirect(entries(slot_t, c * CHUNK, CHUNK)), new[:], ACT.Copy)
 
-        h0 = hidden(pre[0], CHUNK, "h0")
-        h1 = hidden(pre[1], CHUNK, "h1")
-        g0 = look_up(0, CHUNK)
-        h23 = hidden(pre[2], HALF, "h23", 28 * KIB)
-        h2, h3 = h23[:, 0:CHUNK // RUN], h23[:, CHUNK // RUN:]
+        h0 = hidden(0)
+        h1 = hidden(1)
+        h2 = hidden(2)
+        picked0 = look_up(0, CHUNK)
+        picked12 = look_up(CHUNK, HALF)
+        h3 = hidden(3, LAST_HIDDEN_AT)
+        m3 = tile(by_runs, F32, "m3")
+        for t in range(1, PACK):
+            nc.scalar.activation(m3[:, :, t, :], h3[:, :, t, :], ACT.Identity, bias=top_t[:, t:t + 1],
+                                 scale=neg_top[:, t:t + 1])
 
-        m0 = factor(0, h0[:])
+        m0 = whole_factor(0, h0)
         nc.vector.quantize_mx(out=w2_codes[:].bitcast(FP8X4), scales=w2_scales[:], in_=w2_bf[:])
-        z0 = weave(z_tile(0), h0[:], m0[:])
-        m1 = factor(1, h1[:])
+        z0 = weave(z_tile(0), h0, m0)
+        m1 = whole_factor(1, h1)
         y0 = second_product(0, z0)
-        kept0 = dragged(tile([P, CHUNK], F32, "kept0")[:], g0)
-        g12 = look_up(CHUNK, HALF, "mom_g0")
-        m3 = factor(3, h3)
-        z1 = weave(z_tile(1, 32 * KIB), h1[:], m1[:])
-        new0 = kick(0, y0, kept0)
-        put(0, new0)
-        g3 = look_up(3 * CHUNK, CHUNK)
-        y1 = second_product(1, z1)
-        m2 = factor(2, h2)
-        shared = tile([P, 3 * CHUNK], F32, "shared")
-        kept12 = dragged(shared[:, CHUNK:], g12)
-        z2 = weave(z_tile(2), h2, m2[:])
-        new1 = kick(1, y1, kept12[:, 0:CHUNK], 34 * KIB)
-        put(1, new1)
+        z1 = weave(z_tile(1), h1, m1)
+        kept0 = dragged(tile([P, CHUNK], F32, "kept0")[:], picked0)
+        m2 = tile(by_runs, F32, "m2", THIRD_FACTOR_AT)
+        for t in range(PACK):
+            factor(m2, h2, t, last_top[:] if t == PACK - 1 else neg_top[:, t:t + 1])
+        y1 = second_product(1, z1, SECOND_SCALES_AT)
+        put(0, kick(0, y0, kept0))
+        picked3 = look_up(3 * CHUNK, CHUNK)
+        kept_then_z = tile([P, 3 * CHUNK], F32, "kept_then_z")
+        kept12 = dragged(kept_then_z[:, CHUNK:], picked12)
+        z2 = weave(z_tile(2), h2, m2)
+        put(1, kick(1, y1, kept12[:, 0:CHUNK], LAST_TOP_AT))
+        factor(m3, h3, 0, neg_top[:, 0:1])
         y2 = second_product(2, z2)
-        z3 = weave(shared[:, 0:2 * CHUNK].bitcast(BF16), h3, m3[:])
-        new2 = kick(2, y2, kept12[:, CHUNK:])
-        put(2, new2)
+        z3 = weave(kept_then_z[:, 0:HALF].bitcast(BF16), h3, m3)
+        put(2, kick(2, y2, kept12[:, CHUNK:]))
         y3 = second_product(3, z3)
-        kept3 = dragged(tile([P, CHUNK], F32, "kept3", "m3")[:], g3)
-        new3 = kick(3, y3, kept3)
-        put(3, new3)
+        kept3 = dragged(tile([P, CHUNK], F32, "kept3", tag="m3")[:], picked3)
+        put(3, kick(3, y3, kept3))
+
         nc.sync.dma_start(out=out, in_=window[:])

from contextlib import ExitStack

import concourse.mybir as mybir

K, T, S, H, N, U = 1024, 2048, 512, 512, 128, 1024
FLOPS = 2 * K * H * S + 2 * H * N * S

F32 = mybir.dt.float32
BF16 = mybir.dt.bfloat16
I32 = mybir.dt.int32
U32 = mybir.dt.uint32
U16 = mybir.dt.uint16
U8 = mybir.dt.uint8
FP8X4 = mybir.dt.float8_e4m3fn_x4
ACT = mybir.ActivationFunctionType
ALU = mybir.AluOpType

P = 128
PACK = 4
K_PASS = P * PACK
PASSES = K // K_PASS
QUADRANT = 32
SCALE_ROWS = 4
LIST_ROWS = 16
PAIRS = 2
PAIR = PACK // PAIRS
CHUNK = 128
HALF = 2 * CHUNK
RUN = 4
HELPED = 40
KICK = 0.4

KIB = 1024
OVERLAP = 64
LAST_WORDS_AT = 0
SCALE_STAGE_AT = 8 * KIB - OVERLAP
FIRST_ROUNDED_AT = SCALE_STAGE_AT + T - OVERLAP
FIRST_WORDS_AT = 12 * KIB
FIRST_W1_AT = 20 * KIB
DRAG_AT = 32 * KIB - OVERLAP
LAST_HIDDEN_AT = DRAG_AT + OVERLAP - 2 * KIB
SECOND_SCALES_AT = DRAG_AT + OVERLAP
THIRD_FACTOR_AT = SECOND_SCALES_AT + CHUNK
LAST_TOP_AT = 35 * KIB


def tile_picked_yham_drag_p_kernel(
    tc, x_words, x_scales, mom, w1, w2, bias, top, drag, offs, slot, out
):
    nc = tc.nc
    with ExitStack() as ctx:
        sb = ctx.enter_context(tc.tile_pool(name="sb", bufs=1))
        ps = ctx.enter_context(tc.psum_pool(name="ps", bufs=1))
        laid = ctx.enter_context(tc.tile_pool(name="laid", bufs=1))

        def tile(shape, dtype, name, at=None, tag=None):
            if at is None:
                return sb.tile(shape, dtype, name=name, tag=tag or name, align_bytes=64)
            return laid.tile(shape, dtype, name=name, align_bytes=64, offset=at)

        def entries(list_tile, first, count):
            return list_tile[:, first // LIST_ROWS:(first + count) // LIST_ROWS]

        offs_t = sb.tile([P, S // LIST_ROWS], U16, name="offs_t")
        slot_t = sb.tile([P, S // LIST_ROWS], U16, name="slot_t")
        x_word_t = [tile([P, T], U32, "xw0", FIRST_WORDS_AT), tile([P, T], U32, "xw1", LAST_WORDS_AT)]
        x_scale_t = tile([P, T], U8, "xs", SCALE_STAGE_AT)
        w1_first = tile([P, PAIR * P * PACK], BF16, "w1_first", FIRST_ROUNDED_AT)
        table = tile([P, U], F32, "table", FIRST_WORDS_AT)
        window = tile([P, U], F32, "window", FIRST_WORDS_AT + 4 * U)
        w1_raw = [tile([P, PACK, H], F32, "w1_raw0", FIRST_W1_AT), tile([P, PACK, H], F32, "w1_raw1")]
        w2_raw = tile([P, PACK, N], F32, "w2_raw", FIRST_W1_AT)
        picked_rows = tile([P, S], U8, "picked_rows")
        picked_scales = [tile([P, S], U8, f"gs{g}") for g in range(PASSES)]
        bias_t = tile([P, PACK], F32, "bias_t")
        top_t = tile([P, PACK], F32, "top_t")
        drag_t = tile([P, OVERLAP], F32, "drag_t", DRAG_AT)

        def load_w1(g):
            rows = w1[g * K_PASS:(g + 1) * K_PASS, :]
            nc.sync.dma_start(out=w1_raw[g][:], in_=rows.rearrange("(p j) c -> p j c", j=PACK))

        def load_x_words(g):
            nc.sync.dma_start(out=x_word_t[g][:].bitcast(I32),
                              in_=x_words[g].rearrange("p n j -> p (n j)").bitcast(I32))

        def move_scales(g):
            for q in (0, 2, 1, 3):
                first = QUADRANT * q + SCALE_ROWS * g
                nc.sync.dma_start(out=picked_scales[g][QUADRANT * q:QUADRANT * q + SCALE_ROWS, :].bitcast(I32),
                                  in_=picked_rows[first:QUADRANT * (q + 1):PASSES * SCALE_ROWS, :].bitcast(I32))

        nc.vector.memset(x_scale_t[:].bitcast(I32), 0)
        for g in range(PASSES):
            nc.vector.memset(picked_scales[g][:].bitcast(I32), 0)
        load_w1(0)
        nc.sync.dma_start(offs_t[:], offs)
        nc.sync.dma_start(out=x_scale_t[0:P:SCALE_ROWS, :].bitcast(I32),
                          in_=x_scales.rearrange("g b n -> b g n").bitcast(I32))
        load_x_words(0)
        load_w1(1)
        nc.vector.tensor_copy(picked_rows[:], x_scale_t[:].indirect(offs_t[:]))
        move_scales(0)
        load_x_words(1)
        move_scales(1)

        nc.gpsimd.dma_start(out=bias_t[:], in_=bias.rearrange("(p t) o -> p (t o)", t=PACK))
        nc.gpsimd.dma_start(out=top_t[:], in_=top.rearrange("(p t) o -> p (t o)", t=PACK))
        neg_top = tile([P, PACK], F32, "neg_top")
        drag_kick = tile([P, 1], F32, "drag_kick")
        nc.gpsimd.tensor_scalar(neg_top[:], top_t[:], -1.0, 0.0, ALU.mult, ALU.add)
        last_top = tile([P, 1], F32, "last_top", LAST_TOP_AT)
        nc.gpsimd.tensor_scalar(last_top[:], top_t[:, PACK - 1:PACK], -1.0, 0.0, ALU.mult, ALU.add)

        w1_codes = [tile([P, H], U32, f"w1_c{g}") for g in range(PASSES)]
        w1_scales = [tile([P, H], U8, f"w1_s{g}") for g in range(PASSES)]

        def quantise_w1(g, helped):
            src = w1_raw[g][:].rearrange("p j (m u v) -> p u m v j", u=PAIRS, v=PAIR)
            w1_bf = [w1_first if g == 0 and u == 0
                     else tile([P, PAIR * P * PACK], BF16, f"w1_b{g}_{u}") for u in range(PAIRS)]
            dst = [w1_bf[u][:].rearrange("p (v m j) -> p m v j", v=PAIR, j=PACK) for u in range(PAIRS)]
            nc.vector.tensor_copy(dst[0], src[:, 0])
            if helped:
                nc.vector.tensor_copy(dst[1][:, 0:helped], src[:, 1, 0:helped])
            nc.scalar.copy(dst[1][:, helped:], src[:, 1, helped:])
            for u in range(PAIRS):
                cols = slice(u * PAIR * P, (u + 1) * PAIR * P)
                nc.vector.quantize_mx(out=w1_codes[g][:, cols].bitcast(FP8X4), scales=w1_scales[g][:, cols],
                                      in_=w1_bf[u][:])

        picked_words = [tile([P, S], U32, f"gx{g}") for g in range(PASSES)]
        shared_by = (1, PAIR, PACK, PACK)
        banks = [[ps.tile([P, shared, CHUNK], F32, name=f"pre{c}_{b}", tag=f"bank{c}_{b}")
                  for b in range(PACK // shared)] for c, shared in enumerate(shared_by)]
        pre = [[banks[c][t // shared][:, t % shared, :] for t in range(PACK)] for c, shared in enumerate(shared_by)]

        def first_product(g):
            for first, count in ((0, CHUNK), (CHUNK, CHUNK), (HALF, HALF)):
                nc.vector.tensor_copy(picked_words[g][:, first:first + count],
                                      x_word_t[g][:].indirect(entries(offs_t, first, count)))
                for c in range(first // CHUNK, (first + count) // CHUNK):
                    tokens = slice(c * CHUNK, (c + 1) * CHUNK)
                    for t in range(PACK):
                        nc.tensor.matmul_mx(
                            out=pre[c][t],
                            lhsT=w1_codes[g][:, t * P:(t + 1) * P].bitcast(FP8X4),
                            lhsT_scale=w1_scales[g][:, t * P:(t + 1) * P],
                            rhs=picked_words[g][:, tokens].bitcast(FP8X4),
                            rhs_scale=picked_scales[g][:, tokens],
                            start=g == 0 and t % shared_by[c] == 0,
                            stop=g == PASSES - 1 and t % shared_by[c] == shared_by[c] - 1)

        quantise_w1(0, 0)
        first_product(0)
        nc.sync.dma_start(out=w2_raw[:], in_=w2.rearrange("(p j) n -> p j n", j=PACK))
        nc.sync.dma_start(slot_t[:], slot)
        nc.sync.dma_start(out=table[:], in_=mom)
        nc.sync.dma_start(out=drag_t[:, 0:1], in_=drag)
        nc.sync.dma_start(out=window[:], in_=mom)
        quantise_w1(1, HELPED)
        first_product(1)

        w2_bf = tile([P, N * PACK], BF16, "w2_b")
        w2_codes = tile([P, N], U32, "w2_c")
        w2_scales = tile([P, N], U8, "w2_s")
        nc.gpsimd.tensor_scalar(w2_bf[:].rearrange("p (n j) -> p n j", j=PACK), w2_raw[:].rearrange("p j n -> p n j"),
                                1.0, 0.0, ALU.mult, ALU.add)
        nc.gpsimd.tensor_scalar(drag_kick[:], drag_t[:, 0:1], -KICK, 0.0, ALU.mult, ALU.add)

        by_runs = [P, CHUNK // RUN, PACK, RUN]

        def hidden(c, at=None):
            h = tile(by_runs, F32, f"h{c}", at)
            for t in range(PACK):
                nc.scalar.activation(h[:, :, t, :], pre[c][t].rearrange("p (c i) -> p c i", i=RUN), ACT.Tanh,
                                     bias=bias_t[:, t:t + 1])
            return h

        def factor(m, h, t, minus_top):
            nc.vector.tensor_scalar(m[:, :, t, :], h[:, :, t, :], -1.0, minus_top, ALU.add, ALU.mult)

        def whole_factor(c, h):
            m = tile(by_runs, F32, f"m{c}")
            for t in range(PACK):
                factor(m, h, t, neg_top[:, t:t + 1])
            return m

        def z_tile(c):
            return tile([P, CHUNK * PACK], BF16, f"z_b{c}")[:]

        def weave(z_bf, h, m):
            nc.vector.scalar_tensor_tensor(z_bf.rearrange("p (i ct) -> p ct i", i=RUN),
                                           h[:].rearrange("p c t i -> p (c t) i"), 1.0,
                                           m[:].rearrange("p c t i -> p (c t) i"), ALU.add, ALU.mult)
            return z_bf

        def second_product(c, z_bf, scales_at=None):
            z_codes = tile([P, CHUNK], U32, f"z_c{c}")
            z_scales = tile([P, CHUNK], U8, f"z_s{c}", scales_at)
            nc.vector.quantize_mx(out=z_codes[:].bitcast(FP8X4), scales=z_scales[:], in_=z_bf)
            y = ps.tile([P, CHUNK], F32, name=f"y{c}", tag=f"bank0_{c}")
            nc.tensor.matmul_mx(out=y[:], lhsT=w2_codes[:].bitcast(FP8X4), lhsT_scale=w2_scales[:],
                                rhs=z_codes[:].bitcast(FP8X4), rhs_scale=z_scales[:], start=True, stop=True)
            return y

        def look_up(first, count):
            picked = tile([P, count], F32, f"mom_g{first}")
            nc.scalar.activation(picked[:], table[:].indirect(entries(slot_t, first, count)), ACT.Copy)
            return picked

        def dragged(kept, picked):
            nc.vector.tensor_scalar(kept, picked[:], drag_kick[:], -1.0 / KICK, ALU.mult, ALU.mult)
            return kept

        def kick(c, y, kept, at=None):
            new = tile([P, CHUNK], F32, f"new{c}", at)
            nc.vector.scalar_tensor_tensor(new[:].rearrange("p (c i) -> p c i", i=RUN),
                                           y[:].rearrange("p (i c) -> p c i", i=RUN), drag_kick[:],
                                           kept.rearrange("p (c i) -> p c i", i=RUN), ALU.mult, ALU.add)
            return new

        def put(c, new):
            nc.scalar.activation(window[:].indirect(entries(slot_t, c * CHUNK, CHUNK)), new[:], ACT.Copy)

        h0 = hidden(0)
        h1 = hidden(1)
        h2 = hidden(2)
        picked0 = look_up(0, CHUNK)
        picked12 = look_up(CHUNK, HALF)
        h3 = hidden(3, LAST_HIDDEN_AT)
        m3 = tile(by_runs, F32, "m3")
        for t in range(1, PACK):
            nc.scalar.activation(m3[:, :, t, :], h3[:, :, t, :], ACT.Identity, bias=top_t[:, t:t + 1],
                                 scale=neg_top[:, t:t + 1])

        m0 = whole_factor(0, h0)
        nc.vector.quantize_mx(out=w2_codes[:].bitcast(FP8X4), scales=w2_scales[:], in_=w2_bf[:])
        z0 = weave(z_tile(0), h0, m0)
        m1 = whole_factor(1, h1)
        y0 = second_product(0, z0)
        z1 = weave(z_tile(1), h1, m1)
        kept0 = dragged(tile([P, CHUNK], F32, "kept0")[:], picked0)
        m2 = tile(by_runs, F32, "m2", THIRD_FACTOR_AT)
        for t in range(PACK):
            factor(m2, h2, t, last_top[:] if t == PACK - 1 else neg_top[:, t:t + 1])
        y1 = second_product(1, z1, SECOND_SCALES_AT)
        put(0, kick(0, y0, kept0))
        picked3 = look_up(3 * CHUNK, CHUNK)
        kept_then_z = tile([P, 3 * CHUNK], F32, "kept_then_z")
        kept12 = dragged(kept_then_z[:, CHUNK:], picked12)
        z2 = weave(z_tile(2), h2, m2)
        put(1, kick(1, y1, kept12[:, 0:CHUNK], LAST_TOP_AT))
        factor(m3, h3, 0, neg_top[:, 0:1])
        y2 = second_product(2, z2)
        z3 = weave(kept_then_z[:, 0:HALF].bitcast(BF16), h3, m3)
        put(2, kick(2, y2, kept12[:, CHUNK:]))
        y3 = second_product(3, z3)
        kept3 = dragged(tile([P, CHUNK], F32, "kept3", tag="m3")[:], picked3)
        put(3, kick(3, y3, kept3))

        nc.sync.dma_start(out=out, in_=window[:])
